import numpy as np
import ml_dtypes


def mxq(x, axis, fmt="e4m3"):
    dtype, down = {"e4m3": (ml_dtypes.float8_e4m3fn, 7), "e5m2": (ml_dtypes.float8_e5m2, 14)}[fmt]
    v = np.moveaxis(np.asarray(x, np.float32).astype(ml_dtypes.bfloat16).astype(np.float64), axis, -1)
    blocks = v.reshape(v.shape[:-1] + (-1, 32))
    amax = np.abs(blocks).max(-1, keepdims=True)
    byte = np.maximum(np.where(amax > 0, np.frexp(amax)[1] - 1 + 127, 0) - down, 1)
    scale = np.exp2(byte - 127.0)
    codes = (blocks / scale).astype(np.float32).astype(dtype).astype(np.float64)
    return np.moveaxis((codes * scale).reshape(v.shape), -1, axis)


WIDE = False


def mx_kscale(k):
    if not WIDE:
        return np.ones(k)
    levels = np.array([10, -10, 5, -5, 0])
    if k % 512:
        return np.exp2(np.random.permutation(np.resize(levels, k // 32))).repeat(32)
    a = np.empty((k // 512, 16))
    for p in range(k // 512):
        a[p, :8] = np.random.permutation(np.resize(levels, 8))
        for g in range(8):
            far = levels[np.abs(levels - a[p, g]) >= 10]
            a[p, g + 8] = far[np.random.randint(len(far))]
    return np.exp2(a.ravel()).repeat(32)


def f64(x):
    return np.asarray(x).astype(np.float64)


def striped(idx):
    return np.tile(idx.reshape(-1, 16).T, (8, 1)).astype(np.uint16)


def unstriped(offs):
    return offs[:16].T.reshape(-1).astype(np.int64)


def striped8(idx):
    return np.concatenate([x.reshape(-1, 16).T for x in idx]).astype(np.uint16)


def runs(offs, k):
    lists = np.stack([offs[16 * r : 16 * r + 16].T.reshape(-1) for r in range(8)]).astype(np.int64)
    return lists[np.arange(k) % 512 // 64]


def pack_weight(w):
    k, n = w.shape
    w = f64(np.asarray(w, np.float32).astype(ml_dtypes.bfloat16)).reshape(k // 32, 32, n)
    amax = np.abs(w).max(1)
    byte = np.clip(np.where(amax > 0, np.frexp(amax)[1] - 1 + 127 - 7, 1), 1, 254)
    scaled = (w * np.exp2(127.0 - byte)[:, None, :]).reshape(k, n).astype(np.float32)
    words = np.ascontiguousarray(scaled.reshape(k // 512, 128, 4, n).transpose(0, 1, 3, 2)).astype(ml_dtypes.float8_e4m3fn).view(np.uint8)
    return words, np.ascontiguousarray(byte.astype(np.uint8).reshape(k // 512, 16, n))


def unpack_weight(words, scales):
    g, p, n, _ = words.shape
    vals = np.ascontiguousarray(words).view(ml_dtypes.float8_e4m3fn).astype(np.float64) * np.repeat(np.exp2(scales.astype(np.float64) - 127.0), 8, axis=1)[..., None]
    return vals.transpose(0, 1, 3, 2).reshape(g * 512, n)

def planes(y):
    n, m = y.shape
    v = y.astype(np.float32).astype(ml_dtypes.bfloat16).astype(np.float64).reshape(n // 32, 32, m)
    top = np.abs(v).max(1)
    byte = np.clip(np.where(top > 0, np.frexp(top)[1] - 1 + 127 - 7, 1), 1, 254)
    codes = (v * np.exp2(127.0 - byte)[:, None, :]).reshape(n, m).astype(np.float32).astype(ml_dtypes.float8_e4m3fn).view(np.uint8)
    words = codes.reshape(n // 512, 128, 4, m).transpose(0, 1, 3, 2)
    return np.ascontiguousarray(words), np.ascontiguousarray(byte.astype(np.uint8).reshape(n // 512, 16, m))


K, T, S, N, U = 1024, 2048, 512, 512, 1024


def setup_inputs():
    n = np.random.standard_normal
    s = mx_kscale(K)[:, None]
    packed_xT = pack_weight(n((K, T)) * s)
    return {
        "x_words": packed_xT[0],
        "x_scales": packed_xT[1],
        "w1": (n((K, N)) / np.sqrt(K) / s).astype(np.float32),
        "par": n((N, U)).astype(np.float32),
        "offs": striped(np.random.permutation(T)[:S]),
        "ent": striped8(np.stack([np.random.permutation(U)[:S] for _ in range(8)])),
    }


def reference(x_words, x_scales, w1, par, offs, ent):
    o = f64(par)[np.arange(N)[:, None], runs(ent, N)]
    xq = unpack_weight(x_words, x_scales)[:, unstriped(offs)]
    y = mxq(f64(w1), 0, "e4m3").T @ xq
    pn = 0.875 * o - np.clip(y, -0.75, 0.75)
    out = f64(par).copy()
    out[np.arange(N)[:, None], runs(ent, N)] = pn
    return (out,) + planes(out)

@@ -1,0 +1,151 @@
+from contextlib import ExitStack
+
+import concourse.mybir as mybir
+
+K, T, S, N, U = 1024, 2048, 512, 512, 1024
+FLOPS = 2 * K * N * S
+
+F32 = mybir.dt.float32
+BF16 = mybir.dt.bfloat16
+I32 = mybir.dt.int32
+U32 = mybir.dt.uint32
+U16 = mybir.dt.uint16
+U8 = mybir.dt.uint8
+FP8X4 = mybir.dt.float8_e4m3fn_x4
+ALU = mybir.AluOpType
+ACT = mybir.ActivationFunctionType
+
+P = 128
+PACK = 4
+PASSES = K // (P * PACK)
+CHUNK = 256
+CHUNKS = U // CHUNK
+VECTOR_CHUNKS = 2
+
+
+def tile_picked_clipsgd_none_po_kernel(
+    tc, x_words, x_scales, w1, par, offs, ent, out_0, out_1, out_2
+):
+    nc = tc.nc
+    with ExitStack() as ctx:
+        keep = ctx.enter_context(tc.tile_pool(name="keep", bufs=1))
+        psum = ctx.enter_context(tc.psum_pool(name="psum", bufs=1))
+
+        offs_sb = keep.tile([P, S // 16], U16, name="offs_sb")
+        ent_sb = keep.tile([P, S // 16], U16, name="ent_sb")
+        w_raw = [keep.tile([P, PACK, N], F32, name=f"w_raw{z}") for z in range(PASSES)]
+        x_table = [keep.tile([P, T], U32, name=f"x_table{z}", align_bytes=64) for z in range(PASSES)]
+        x_scale_table = keep.tile([P, T], U8, name="x_scale_table", align_bytes=64)
+        rows = [keep.tile([P, U], F32, name=f"rows{t}", align_bytes=64) for t in range(PACK)]
+
+        nc.vector.memset(x_scale_table[:].bitcast(I32), 0)
+        w_passes = w1.rearrange("(z p j) c -> z p j c", z=PASSES, j=PACK)
+        nc.sync.dma_start(out=w_raw[0][:], in_=w_passes[0])
+        for q in range(4):
+            nc.sync.dma_start(
+                out=x_scale_table[32 * q : 32 * q + 4 * PASSES, :].bitcast(I32),
+                in_=x_scales[:, 4 * q : 4 * q + 4, :].bitcast(I32),
+            )
+        nc.sync.dma_start(offs_sb[:], offs)
+        nc.sync.dma_start(ent_sb[:], ent)
+        nc.sync.dma_start(out=w_raw[1][:], in_=w_passes[1])
+        for z in range(PASSES):
+            nc.sync.dma_start(
+                out=x_table[z][:].bitcast(I32),
+                in_=x_words[z].rearrange("p c r -> p (c r)").bitcast(I32),
+            )
+        par_rows = par.rearrange("(p t) c -> t p c", t=PACK)
+        for t in range(PACK):
+            nc.sync.dma_start(out=rows[t][:], in_=par_rows[t])
+
+        x_scale = keep.tile([P, S], U8, name="x_scale", align_bytes=64)
+        nc.vector.tensor_copy(x_scale[:], x_scale_table[:].indirect(offs_sb[:]))
+
+        w_codes, w_scale = [], []
+        for z in range(PASSES):
+            w_bf = keep.tile([P, PACK, P, PACK], BF16, name=f"w_bf{z}", align_bytes=64)
+            dealt = w_bf[:].rearrange("p t m j -> p m j t")
+            source = w_raw[z][:].rearrange("p j (m t) -> p m j t", t=PACK)
+            if z == 0:
+                nc.scalar.copy(out=dealt, in_=source)
+            else:
+                nc.vector.tensor_copy(out=dealt, in_=source)
+            codes = keep.tile([P, N], U32, name=f"w_codes{z}", align_bytes=64)
+            scale = keep.tile([P, N], U8, name=f"w_scale{z}", align_bytes=64)
+            nc.vector.quantize_mx(
+                out=codes[:].bitcast(FP8X4),
+                scales=scale[:],
+                in_=w_bf[:].rearrange("p t m j -> p (t m j)"),
+            )
+            w_codes.append(codes)
+            w_scale.append(scale)
+
+        y = [psum.tile([P, S], F32, name=f"y{t}") for t in range(PACK)]
+        for z in range(PASSES):
+            x_codes = keep.tile([P, S], U32, name=f"x_codes{z}", align_bytes=64)
+            nc.vector.tensor_copy(x_codes[:], x_table[z][:].indirect(offs_sb[:]))
+            for t in range(PACK):
+                cols = slice(P * t, P * (t + 1))
+                nc.tensor.matmul_mx(
+                    out=y[t][:],
+                    lhsT=w_codes[z][:, cols].bitcast(FP8X4),
+                    lhsT_scale=w_scale[z][:, cols],
+                    rhs=x_codes[:].bitcast(FP8X4),
+                    rhs_scale=x_scale[4 * z :, :],
+                    start=(z == 0),
+                    stop=(z == PASSES - 1),
+                )
+
+        minus_y = [keep.tile([P, S], F32, name=f"minus_y{t}") for t in range(PACK)]
+        for t in range(PACK):
+            nc.scalar.activation(out=minus_y[t][:], in_=y[t][:], func=ACT.Copy, scale=-1.0)
+
+        grouped = [
+            keep.tile([P, CHUNK, PACK], BF16, name=f"grouped{c}", align_bytes=64) for c in range(CHUNKS)
+        ]
+        out_rows = out_0.rearrange("(p t) c -> t p c", t=PACK)
+        for t in range(PACK):
+            decayed = keep.tile([P, S], F32, name=f"decayed{t}")
+            nc.vector.tensor_scalar(decayed[:], rows[t][:].indirect(ent_sb[:]), 0.875, 0.0, ALU.mult, ALU.add)
+            step = keep.tile([P, S], F32, name=f"step{t}")
+            nc.vector.tensor_scalar(step[:], minus_y[t][:], 0.75, -0.75, ALU.min, ALU.max)
+            nc.vector.tensor_tensor(rows[t][:].indirect(ent_sb[:]), decayed[:], step[:], ALU.add)
+            nc.sync.dma_start(out=out_rows[t], in_=rows[t][:])
+            if t == PACK - 1:
+                break
+            for c in range(CHUNKS):
+                part = rows[t][:, c * CHUNK : (c + 1) * CHUNK]
+                if t == PACK - 2 and c < VECTOR_CHUNKS:
+                    nc.scalar.copy(
+                        out=grouped[c][:, :, t : t + 2], in_=part.unsqueeze(2).to_broadcast([P, CHUNK, 2])
+                    )
+                else:
+                    nc.scalar.copy(out=grouped[c][:, :, t], in_=part)
+
+        last = PACK - 1
+        for c in range(CHUNKS):
+            part = rows[last][:, c * CHUNK : (c + 1) * CHUNK]
+            if c < VECTOR_CHUNKS:
+                nc.vector.tensor_copy(out=grouped[c][:, :, last], in_=part)
+            else:
+                nc.scalar.copy(out=grouped[c][:, :, last], in_=part)
+
+        out_codes = keep.tile([P, U], U32, name="out_codes", align_bytes=64)
+        out_scale = keep.tile([P, U], U8, name="out_scale", align_bytes=64)
+        out_words = out_1[0].rearrange("p c r -> p (c r)").bitcast(I32)
+        for c in range(CHUNKS):
+            cols = slice(c * CHUNK, (c + 1) * CHUNK)
+            nc.vector.quantize_mx(
+                out=out_codes[:, cols].bitcast(FP8X4),
+                scales=out_scale[:, cols],
+                in_=grouped[c][:].rearrange("p c t -> p (c t)"),
+            )
+            if c >= VECTOR_CHUNKS - 1:
+                done = slice(0 if c < VECTOR_CHUNKS else c * CHUNK, (c + 1) * CHUNK)
+                nc.sync.dma_start(out=out_words[:, done], in_=out_codes[:, done].bitcast(I32))
+        for q in range(4):
+            queue = nc.scalar if q % 2 else nc.sync
+            queue.dma_start(
+                out=out_2[0, 4 * q : 4 * q + 4, :].bitcast(I32),
+                in_=out_scale[32 * q : 32 * q + 4, :].bitcast(I32),
+            )

@@ -21,6 +21,7 @@ PASSES = K // (P * PACK)
 CHUNK = 256
 CHUNKS = U // CHUNK
 VECTOR_CHUNKS = 2
+EDGE = 8
 
 
 def tile_picked_clipsgd_none_po_kernel(
@@ -55,7 +56,7 @@ def tile_picked_clipsgd_none_po_kernel(
                 in_=x_words[z].rearrange("p c r -> p (c r)").bitcast(I32),
             )
         par_rows = par.rearrange("(p t) c -> t p c", t=PACK)
-        for t in range(PACK):
+        for t in (1, 0, 2, 3):
             nc.sync.dma_start(out=rows[t][:], in_=par_rows[t])
 
         x_scale = keep.tile([P, S], U8, name="x_scale", align_bytes=64)
@@ -84,7 +85,7 @@ def tile_picked_clipsgd_none_po_kernel(
         for z in range(PASSES):
             x_codes = keep.tile([P, S], U32, name=f"x_codes{z}", align_bytes=64)
             nc.vector.tensor_copy(x_codes[:], x_table[z][:].indirect(offs_sb[:]))
-            for t in range(PACK):
+            for t in (0, 2, 3, 1):
                 cols = slice(P * t, P * (t + 1))
                 nc.tensor.matmul_mx(
                     out=y[t][:],
@@ -97,27 +98,31 @@ def tile_picked_clipsgd_none_po_kernel(
                 )
 
         minus_y = [keep.tile([P, S], F32, name=f"minus_y{t}") for t in range(PACK)]
-        for t in range(PACK):
+        for t in (0, 2, 3, 1):
             nc.scalar.activation(out=minus_y[t][:], in_=y[t][:], func=ACT.Copy, scale=-1.0)
+        steps = [keep.tile([P, S], F32, name=f"step{t}") for t in range(PACK)]
+        for t in (0, 2, 3, 1):
+            nc.gpsimd.tensor_scalar(steps[t][:], minus_y[t][:], 0.75, -0.75, ALU.min, ALU.max)
 
         grouped = [
             keep.tile([P, CHUNK, PACK], BF16, name=f"grouped{c}", align_bytes=64) for c in range(CHUNKS)
         ]
+        decayed = [keep.tile([P, S], F32, name=f"decayed{t}") for t in range(PACK)]
+        for t in (1, 0, 2, 3):
+            nc.vector.tensor_scalar(decayed[t][:], rows[t][:].indirect(ent_sb[:]), 0.875, 0.0, ALU.mult, ALU.add)
         out_rows = out_0.rearrange("(p t) c -> t p c", t=PACK)
         for t in range(PACK):
-            decayed = keep.tile([P, S], F32, name=f"decayed{t}")
-            nc.vector.tensor_scalar(decayed[:], rows[t][:].indirect(ent_sb[:]), 0.875, 0.0, ALU.mult, ALU.add)
-            step = keep.tile([P, S], F32, name=f"step{t}")
-            nc.vector.tensor_scalar(step[:], minus_y[t][:], 0.75, -0.75, ALU.min, ALU.max)
-            nc.vector.tensor_tensor(rows[t][:].indirect(ent_sb[:]), decayed[:], step[:], ALU.add)
+            nc.vector.tensor_tensor(rows[t][:].indirect(ent_sb[:]), decayed[t][:], steps[t][:], ALU.add)
             nc.sync.dma_start(out=out_rows[t], in_=rows[t][:])
             if t == PACK - 1:
                 break
             for c in range(CHUNKS):
                 part = rows[t][:, c * CHUNK : (c + 1) * CHUNK]
                 if t == PACK - 2 and c < VECTOR_CHUNKS:
+                    nc.scalar.copy(out=grouped[c][:, EDGE:, t], in_=part[:, EDGE:])
                     nc.scalar.copy(
-                        out=grouped[c][:, :, t : t + 2], in_=part.unsqueeze(2).to_broadcast([P, CHUNK, 2])
+                        out=grouped[c][:, :EDGE, t : t + 2],
+                        in_=part[:, :EDGE].unsqueeze(2).to_broadcast([P, EDGE, 2]),
                     )
                 else:
                     nc.scalar.copy(out=grouped[c][:, :, t], in_=part)

@@ -22,6 +22,7 @@ CHUNK = 256
 CHUNKS = U // CHUNK
 VECTOR_CHUNKS = 2
 EDGE = 8
+W_BYTES = 4 * PACK * N
 
 
 def tile_picked_clipsgd_none_po_kernel(
@@ -34,40 +35,49 @@ def tile_picked_clipsgd_none_po_kernel(
 
         offs_sb = keep.tile([P, S // 16], U16, name="offs_sb")
         ent_sb = keep.tile([P, S // 16], U16, name="ent_sb")
-        w_raw = [keep.tile([P, PACK, N], F32, name=f"w_raw{z}") for z in range(PASSES)]
-        x_table = [keep.tile([P, T], U32, name=f"x_table{z}", align_bytes=64) for z in range(PASSES)]
-        x_scale_table = keep.tile([P, T], U8, name="x_scale_table", align_bytes=64)
-        rows = [keep.tile([P, U], F32, name=f"rows{t}", align_bytes=64) for t in range(PACK)]
+        early = ctx.enter_context(tc.tile_pool(name="early", bufs=1))
+        w_raw = [early.tile([P, PACK, N], F32, name=f"w_raw{z}", offset=z * W_BYTES) for z in range(PASSES)]
+        x_scale_table = early.tile([P, PASSES, T], U8, name="x_scale_table", offset=PASSES * W_BYTES)
+        x_first = keep.tile([P, T], U32, name="x_table0", align_bytes=64)
+        x_picked_scale = keep.tile([P, PASSES, S], U8, name="x_picked_scale", align_bytes=64)
+        x_scale = keep.tile([P, PASSES, S], U8, name="x_scale", align_bytes=64)
 
-        nc.vector.memset(x_scale_table[:].bitcast(I32), 0)
-        w_passes = w1.rearrange("(z p j) c -> z p j c", z=PASSES, j=PACK)
-        nc.sync.dma_start(out=w_raw[0][:], in_=w_passes[0])
-        for q in range(4):
+        def load_x(table, z):
             nc.sync.dma_start(
-                out=x_scale_table[32 * q : 32 * q + 4 * PASSES, :].bitcast(I32),
-                in_=x_scales[:, 4 * q : 4 * q + 4, :].bitcast(I32),
-            )
-        nc.sync.dma_start(offs_sb[:], offs)
-        nc.sync.dma_start(ent_sb[:], ent)
-        nc.sync.dma_start(out=w_raw[1][:], in_=w_passes[1])
-        for z in range(PASSES):
-            nc.sync.dma_start(
-                out=x_table[z][:].bitcast(I32),
+                out=table[:].bitcast(I32),
                 in_=x_words[z].rearrange("p c r -> p (c r)").bitcast(I32),
             )
-        par_rows = par.rearrange("(p t) c -> t p c", t=PACK)
-        for t in (1, 0, 2, 3):
-            nc.sync.dma_start(out=rows[t][:], in_=par_rows[t])
 
-        x_scale = keep.tile([P, S], U8, name="x_scale", align_bytes=64)
-        nc.vector.tensor_copy(x_scale[:], x_scale_table[:].indirect(offs_sb[:]))
+        nc.vector.memset(x_scale_table[:].rearrange("p z c -> p (z c)").bitcast(I32), 0)
+        nc.vector.memset(x_scale[:].rearrange("p z c -> p (z c)").bitcast(I32), 0)
+        w_passes = w1.rearrange("(z p j) c -> z p j c", z=PASSES, j=PACK)
+        nc.sync.dma_start(out=w_raw[0][:, :2, :], in_=w_passes[0][:, :2, :])
+        nc.sync.dma_start(
+            out=x_scale_table[32:96:4].bitcast(I32),
+            in_=x_scales.rearrange("z q c -> q z c").bitcast(I32),
+        )
+        nc.sync.dma_start(offs_sb[:], offs)
+        nc.sync.dma_start(out=w_raw[0][:, 2:, :], in_=w_passes[0][:, 2:, :])
+        nc.sync.dma_start(out=w_raw[1][:], in_=w_passes[1])
+        load_x(x_first, 0)
+        nc.sync.dma_start(ent_sb[:], ent)
+        for z in range(PASSES):
+            nc.vector.tensor_copy(x_picked_scale[:, z, :], x_scale_table[:, z, :].indirect(offs_sb[:]))
+        for q in range(4):
+            nc.sync.dma_start(
+                out=x_scale[32 * q : 32 * q + 4].rearrange("p z c -> p (z c)").bitcast(I32),
+                in_=x_picked_scale[32 + 16 * q : 48 + 16 * q : 4].rearrange("p z c -> p (z c)").bitcast(I32),
+            )
+        x_last = early.tile([P, T], U32, name="x_table1", offset=PASSES * W_BYTES)
+        load_x(x_last, 1)
+        x_table = [x_first, x_last]
 
         w_codes, w_scale = [], []
         for z in range(PASSES):
             w_bf = keep.tile([P, PACK, P, PACK], BF16, name=f"w_bf{z}", align_bytes=64)
             dealt = w_bf[:].rearrange("p t m j -> p m j t")
             source = w_raw[z][:].rearrange("p j (m t) -> p m j t", t=PACK)
-            if z == 0:
+            if z == 1:
                 nc.scalar.copy(out=dealt, in_=source)
             else:
                 nc.vector.tensor_copy(out=dealt, in_=source)
@@ -81,39 +91,54 @@ def tile_picked_clipsgd_none_po_kernel(
             w_codes.append(codes)
             w_scale.append(scale)
 
+        rows = {}
+        par_rows = par.rearrange("(p t) c -> t p c", t=PACK)
+        for place, t in enumerate((1, 0, 2, 3)):
+            rows[t] = early.tile([P, U], F32, name=f"rows{t}", offset=place * 4 * U)
+            nc.sync.dma_start(out=rows[t][:], in_=par_rows[t])
+
         y = [psum.tile([P, S], F32, name=f"y{t}") for t in range(PACK)]
         for z in range(PASSES):
             x_codes = keep.tile([P, S], U32, name=f"x_codes{z}", align_bytes=64)
             nc.vector.tensor_copy(x_codes[:], x_table[z][:].indirect(offs_sb[:]))
-            for t in (0, 2, 3, 1):
+            for t in range(PACK):
                 cols = slice(P * t, P * (t + 1))
                 nc.tensor.matmul_mx(
                     out=y[t][:],
                     lhsT=w_codes[z][:, cols].bitcast(FP8X4),
                     lhsT_scale=w_scale[z][:, cols],
                     rhs=x_codes[:].bitcast(FP8X4),
-                    rhs_scale=x_scale[4 * z :, :],
+                    rhs_scale=x_scale[:, z, :],
                     start=(z == 0),
                     stop=(z == PASSES - 1),
                 )
 
         minus_y = [keep.tile([P, S], F32, name=f"minus_y{t}") for t in range(PACK)]
-        for t in (0, 2, 3, 1):
+        for t in range(PACK):
             nc.scalar.activation(out=minus_y[t][:], in_=y[t][:], func=ACT.Copy, scale=-1.0)
-        steps = [keep.tile([P, S], F32, name=f"step{t}") for t in range(PACK)]
-        for t in (0, 2, 3, 1):
-            nc.gpsimd.tensor_scalar(steps[t][:], minus_y[t][:], 0.75, -0.75, ALU.min, ALU.max)
+        steps = {}
+
+        def clip(engine, t, tag):
+            steps[t] = keep.tile([P, S], F32, name=f"step{t}", tag=tag)
+            engine.tensor_scalar(steps[t][:], minus_y[t][:], 0.75, -0.75, ALU.min, ALU.max)
+
+        clip(nc.gpsimd, 0, "step_first")
 
         grouped = [
             keep.tile([P, CHUNK, PACK], BF16, name=f"grouped{c}", align_bytes=64) for c in range(CHUNKS)
         ]
-        decayed = [keep.tile([P, S], F32, name=f"decayed{t}") for t in range(PACK)]
+        decayed = [keep.tile([P, S], F32, name=f"decayed{t}", tag=f"decayed{t}") for t in range(PACK)]
         for t in (1, 0, 2, 3):
             nc.vector.tensor_scalar(decayed[t][:], rows[t][:].indirect(ent_sb[:]), 0.875, 0.0, ALU.mult, ALU.add)
         out_rows = out_0.rearrange("(p t) c -> t p c", t=PACK)
         for t in range(PACK):
             nc.vector.tensor_tensor(rows[t][:].indirect(ent_sb[:]), decayed[t][:], steps[t][:], ALU.add)
             nc.sync.dma_start(out=out_rows[t], in_=rows[t][:])
+            if t == 0:
+                clip(nc.gpsimd, 1, "step_first")
+            if t == 1:
+                clip(nc.gpsimd, 2, "step_first")
+                clip(nc.gpsimd, 3, "decayed1")
             if t == PACK - 1:
                 break
             for c in range(CHUNKS):

@@ -22,6 +22,8 @@ CHUNK = 256
 CHUNKS = U // CHUNK
 VECTOR_CHUNKS = 2
 EDGE = 8
+FILL = 160
+HELD = 256
 W_BYTES = 4 * PACK * N
 
 
@@ -101,7 +103,7 @@ def tile_picked_clipsgd_none_po_kernel(
         for z in range(PASSES):
             x_codes = keep.tile([P, S], U32, name=f"x_codes{z}", align_bytes=64)
             nc.vector.tensor_copy(x_codes[:], x_table[z][:].indirect(offs_sb[:]))
-            for t in range(PACK):
+            for t in (0, 3, 1, 2):
                 cols = slice(P * t, P * (t + 1))
                 nc.tensor.matmul_mx(
                     out=y[t][:],
@@ -113,16 +115,22 @@ def tile_picked_clipsgd_none_po_kernel(
                     stop=(z == PASSES - 1),
                 )
 
-        minus_y = [keep.tile([P, S], F32, name=f"minus_y{t}") for t in range(PACK)]
-        for t in range(PACK):
-            nc.scalar.activation(out=minus_y[t][:], in_=y[t][:], func=ACT.Copy, scale=-1.0)
-        steps = {}
+        minus_pair = keep.tile([P, 2 * S], F32, name="minus_pair")
+        minus_y = [keep.tile([P, S], F32, name=f"minus_y{t}")[:] for t in range(2)]
+        minus_y = minus_y + [minus_pair[:, S:], minus_pair[:, :S]]
 
-        def clip(engine, t, tag):
-            steps[t] = keep.tile([P, S], F32, name=f"step{t}", tag=tag)
-            engine.tensor_scalar(steps[t][:], minus_y[t][:], 0.75, -0.75, ALU.min, ALU.max)
+        def turn_sign(t):
+            nc.scalar.activation(out=minus_y[t], in_=y[t][:], func=ACT.Copy, scale=-1.0)
 
-        clip(nc.gpsimd, 0, "step_first")
+        for t in (0, 3, 1):
+            turn_sign(t)
+        steps = keep.tile([P, 2 * S], F32, name="steps")
+
+        def clip(engine, out, in_):
+            engine.tensor_scalar(out, in_, 0.75, -0.75, ALU.min, ALU.max)
+
+        clip(nc.gpsimd, minus_y[2], minus_y[0])
+        clip(nc.gpsimd, steps[:, : S - HELD], minus_pair[:, : S - HELD])
 
         grouped = [
             keep.tile([P, CHUNK, PACK], BF16, name=f"grouped{c}", align_bytes=64) for c in range(CHUNKS)
@@ -130,29 +138,33 @@ def tile_picked_clipsgd_none_po_kernel(
         decayed = [keep.tile([P, S], F32, name=f"decayed{t}", tag=f"decayed{t}") for t in range(PACK)]
         for t in (1, 0, 2, 3):
             nc.vector.tensor_scalar(decayed[t][:], rows[t][:].indirect(ent_sb[:]), 0.875, 0.0, ALU.mult, ALU.add)
+        step = [minus_y[2], decayed[0][:], steps[:, S:], steps[:, :S]]
         out_rows = out_0.rearrange("(p t) c -> t p c", t=PACK)
         for t in range(PACK):
-            nc.vector.tensor_tensor(rows[t][:].indirect(ent_sb[:]), decayed[t][:], steps[t][:], ALU.add)
+            nc.vector.tensor_tensor(rows[t][:].indirect(ent_sb[:]), decayed[t][:], step[t], ALU.add)
             nc.sync.dma_start(out=out_rows[t], in_=rows[t][:])
             if t == 0:
-                clip(nc.gpsimd, 1, "step_first")
-            if t == 1:
-                clip(nc.gpsimd, 2, "step_first")
-                clip(nc.gpsimd, 3, "decayed1")
+                clip(nc.gpsimd, step[1], minus_y[1])
             if t == PACK - 1:
                 break
             for c in range(CHUNKS):
                 part = rows[t][:, c * CHUNK : (c + 1) * CHUNK]
                 if t == PACK - 2 and c < VECTOR_CHUNKS:
-                    nc.scalar.copy(out=grouped[c][:, EDGE:, t], in_=part[:, EDGE:])
+                    first = FILL if c == 0 else 0
+                    edge = CHUNK - EDGE
+                    nc.scalar.copy(out=grouped[c][:, first:edge, t], in_=part[:, first:edge])
                     nc.scalar.copy(
-                        out=grouped[c][:, :EDGE, t : t + 2],
-                        in_=part[:, :EDGE].unsqueeze(2).to_broadcast([P, EDGE, 2]),
+                        out=grouped[c][:, edge:, t : t + 2],
+                        in_=part[:, edge:].unsqueeze(2).to_broadcast([P, EDGE, 2]),
                     )
                 else:
                     nc.scalar.copy(out=grouped[c][:, :, t], in_=part)
+                if t == 0 and c == 0:
+                    turn_sign(2)
+                    clip(nc.gpsimd, steps[:, S - HELD :], minus_pair[:, S - HELD :])
 
         last = PACK - 1
+        nc.vector.tensor_copy(out=grouped[0][:, :FILL, last - 1], in_=rows[last - 1][:, :FILL])
         for c in range(CHUNKS):
             part = rows[last][:, c * CHUNK : (c + 1) * CHUNK]
             if c < VECTOR_CHUNKS:

@@ -115,22 +115,26 @@ def tile_picked_clipsgd_none_po_kernel(
                     stop=(z == PASSES - 1),
                 )
 
-        minus_pair = keep.tile([P, 2 * S], F32, name="minus_pair")
-        minus_y = [keep.tile([P, S], F32, name=f"minus_y{t}")[:] for t in range(2)]
-        minus_y = minus_y + [minus_pair[:, S:], minus_pair[:, :S]]
+        minus_all = keep.tile([P, 2 * S + HELD], F32, name="minus_all")
+        minus_pair = minus_all[:, HELD:]
+        minus_first = keep.tile([P, S], F32, name="minus_first")
+        minus_y = [minus_first[:], minus_all[:, :S], minus_pair[:, S:], minus_pair[:, :S]]
 
         def turn_sign(t):
             nc.scalar.activation(out=minus_y[t], in_=y[t][:], func=ACT.Copy, scale=-1.0)
 
-        for t in (0, 3, 1):
+        for t in (0, 3):
             turn_sign(t)
         steps = keep.tile([P, 2 * S], F32, name="steps")
+        second_step = keep.tile([P, S], F32, name="second_step")
 
         def clip(engine, out, in_):
             engine.tensor_scalar(out, in_, 0.75, -0.75, ALU.min, ALU.max)
 
         clip(nc.gpsimd, minus_y[2], minus_y[0])
         clip(nc.gpsimd, steps[:, : S - HELD], minus_pair[:, : S - HELD])
+        turn_sign(1)
+        clip(nc.gpsimd, second_step[:], minus_y[1])
 
         grouped = [
             keep.tile([P, CHUNK, PACK], BF16, name=f"grouped{c}", align_bytes=64) for c in range(CHUNKS)
@@ -138,13 +142,11 @@ def tile_picked_clipsgd_none_po_kernel(
         decayed = [keep.tile([P, S], F32, name=f"decayed{t}", tag=f"decayed{t}") for t in range(PACK)]
         for t in (1, 0, 2, 3):
             nc.vector.tensor_scalar(decayed[t][:], rows[t][:].indirect(ent_sb[:]), 0.875, 0.0, ALU.mult, ALU.add)
-        step = [minus_y[2], decayed[0][:], steps[:, S:], steps[:, :S]]
+        step = [minus_y[2], second_step[:], steps[:, S:], steps[:, :S]]
         out_rows = out_0.rearrange("(p t) c -> t p c", t=PACK)
         for t in range(PACK):
             nc.vector.tensor_tensor(rows[t][:].indirect(ent_sb[:]), decayed[t][:], step[t], ALU.add)
             nc.sync.dma_start(out=out_rows[t], in_=rows[t][:])
-            if t == 0:
-                clip(nc.gpsimd, step[1], minus_y[1])
             if t == PACK - 1:
                 break
             for c in range(CHUNKS):

@@ -39,9 +39,9 @@ def tile_picked_clipsgd_none_po_kernel(
         ent_sb = keep.tile([P, S // 16], U16, name="ent_sb")
         early = ctx.enter_context(tc.tile_pool(name="early", bufs=1))
         w_raw = [early.tile([P, PACK, N], F32, name=f"w_raw{z}", offset=z * W_BYTES) for z in range(PASSES)]
-        x_scale_table = early.tile([P, PASSES, T], U8, name="x_scale_table", offset=PASSES * W_BYTES)
+        x_scale_table = early.tile([P, T], U8, name="x_scale_table", offset=PASSES * W_BYTES)
         x_first = keep.tile([P, T], U32, name="x_table0", align_bytes=64)
-        x_picked_scale = keep.tile([P, PASSES, S], U8, name="x_picked_scale", align_bytes=64)
+        x_picked_scale = keep.tile([P, S], U8, name="x_picked_scale", align_bytes=64)
         x_scale = keep.tile([P, PASSES, S], U8, name="x_scale", align_bytes=64)
 
         def load_x(table, z):
@@ -50,12 +50,12 @@ def tile_picked_clipsgd_none_po_kernel(
                 in_=x_words[z].rearrange("p c r -> p (c r)").bitcast(I32),
             )
 
-        nc.vector.memset(x_scale_table[:].rearrange("p z c -> p (z c)").bitcast(I32), 0)
+        nc.vector.memset(x_scale_table[:].bitcast(I32), 0)
         nc.vector.memset(x_scale[:].rearrange("p z c -> p (z c)").bitcast(I32), 0)
         w_passes = w1.rearrange("(z p j) c -> z p j c", z=PASSES, j=PACK)
         nc.sync.dma_start(out=w_raw[0][:, :2, :], in_=w_passes[0][:, :2, :])
         nc.sync.dma_start(
-            out=x_scale_table[32:96:4].bitcast(I32),
+            out=x_scale_table[0:128:4].bitcast(I32),
             in_=x_scales.rearrange("z q c -> q z c").bitcast(I32),
         )
         nc.sync.dma_start(offs_sb[:], offs)
@@ -63,13 +63,16 @@ def tile_picked_clipsgd_none_po_kernel(
         nc.sync.dma_start(out=w_raw[1][:], in_=w_passes[1])
         load_x(x_first, 0)
         nc.sync.dma_start(ent_sb[:], ent)
-        for z in range(PASSES):
-            nc.vector.tensor_copy(x_picked_scale[:, z, :], x_scale_table[:, z, :].indirect(offs_sb[:]))
-        for q in range(4):
-            nc.sync.dma_start(
-                out=x_scale[32 * q : 32 * q + 4].rearrange("p z c -> p (z c)").bitcast(I32),
-                in_=x_picked_scale[32 + 16 * q : 48 + 16 * q : 4].rearrange("p z c -> p (z c)").bitcast(I32),
-            )
+        nc.vector.tensor_copy(x_picked_scale[:], x_scale_table[:].indirect(offs_sb[:]))
+
+        def move_scales(z):
+            for q in range(4):
+                nc.sync.dma_start(
+                    out=x_scale[32 * q : 32 * q + 4, z, :].bitcast(I32),
+                    in_=x_picked_scale[32 * q + 4 * z : 32 * q + 32 : 8].bitcast(I32),
+                )
+
+        move_scales(0)
         x_last = early.tile([P, T], U32, name="x_table1", offset=PASSES * W_BYTES)
         load_x(x_last, 1)
         x_table = [x_first, x_last]
@@ -95,9 +98,11 @@ def tile_picked_clipsgd_none_po_kernel(
 
         rows = {}
         par_rows = par.rearrange("(p t) c -> t p c", t=PACK)
-        for place, t in enumerate((1, 0, 2, 3)):
+        for place, t in enumerate((0, 1, 2, 3)):
             rows[t] = early.tile([P, U], F32, name=f"rows{t}", offset=place * 4 * U)
             nc.sync.dma_start(out=rows[t][:], in_=par_rows[t])
+            if t == 0:
+                move_scales(1)
 
         y = [psum.tile([P, S], F32, name=f"y{t}") for t in range(PACK)]
         for z in range(PASSES):
@@ -140,7 +145,7 @@ def tile_picked_clipsgd_none_po_kernel(
             keep.tile([P, CHUNK, PACK], BF16, name=f"grouped{c}", align_bytes=64) for c in range(CHUNKS)
         ]
         decayed = [keep.tile([P, S], F32, name=f"decayed{t}", tag=f"decayed{t}") for t in range(PACK)]
-        for t in (1, 0, 2, 3):
+        for t in (0, 1, 2, 3):
             nc.vector.tensor_scalar(decayed[t][:], rows[t][:].indirect(ent_sb[:]), 0.875, 0.0, ALU.mult, ALU.add)
         step = [minus_y[2], second_step[:], steps[:, S:], steps[:, :S]]
         out_rows = out_0.rearrange("(p t) c -> t p c", t=PACK)

@@ -65,14 +65,18 @@ def tile_picked_clipsgd_none_po_kernel(
         nc.sync.dma_start(ent_sb[:], ent)
         nc.vector.tensor_copy(x_picked_scale[:], x_scale_table[:].indirect(offs_sb[:]))
 
-        def move_scales(z):
-            for q in range(4):
-                nc.sync.dma_start(
-                    out=x_scale[32 * q : 32 * q + 4, z, :].bitcast(I32),
-                    in_=x_picked_scale[32 * q + 4 * z : 32 * q + 32 : 8].bitcast(I32),
-                )
+        def move_last_quadrant(z):
+            nc.sync.dma_start(
+                out=x_scale[96:100, z, :].bitcast(I32),
+                in_=x_picked_scale[96 + 4 * z : 128 : 8].bitcast(I32),
+            )
 
-        move_scales(0)
+        for q in range(3):
+            nc.sync.dma_start(
+                out=x_scale[32 * q : 32 * q + 4].bitcast(I32),
+                in_=x_picked_scale[32 * q : 32 * q + 32 : 4].bitcast(I32),
+            )
+        move_last_quadrant(0)
         x_last = early.tile([P, T], U32, name="x_table1", offset=PASSES * W_BYTES)
         load_x(x_last, 1)
         x_table = [x_first, x_last]
@@ -102,44 +106,60 @@ def tile_picked_clipsgd_none_po_kernel(
             rows[t] = early.tile([P, U], F32, name=f"rows{t}", offset=place * 4 * U)
             nc.sync.dma_start(out=rows[t][:], in_=par_rows[t])
             if t == 0:
-                move_scales(1)
+                move_last_quadrant(1)
 
-        y = [psum.tile([P, S], F32, name=f"y{t}") for t in range(PACK)]
+        halves = [slice(0, S // 2), slice(S // 2, S)]
+        y_first = [psum.tile([P, S // 2], F32, name=f"y_first{h}", tag=f"bank{h}") for h in range(2)]
+        y = {3: psum.tile([P, S], F32, name="y3")}
+        x_codes = [keep.tile([P, S], U32, name=f"x_codes{z}", align_bytes=64) for z in range(PASSES)]
+
+        def multiply(t, bank, picked, z):
+            cols = slice(P * t, P * (t + 1))
+            nc.tensor.matmul_mx(
+                out=bank[:],
+                lhsT=w_codes[z][:, cols].bitcast(FP8X4),
+                lhsT_scale=w_scale[z][:, cols],
+                rhs=x_codes[z][:, picked].bitcast(FP8X4),
+                rhs_scale=x_scale[:, z, picked],
+                start=(z == 0),
+                stop=(z == PASSES - 1),
+            )
+
+        def multiply_late(t):
+            y[t] = psum.tile([P, S], F32, name=f"y{t}", tag=f"bank{t - 1}")
+            for z in range(PASSES):
+                multiply(t, y[t], slice(0, S), z)
+
         for z in range(PASSES):
-            x_codes = keep.tile([P, S], U32, name=f"x_codes{z}", align_bytes=64)
-            nc.vector.tensor_copy(x_codes[:], x_table[z][:].indirect(offs_sb[:]))
-            for t in (0, 3, 1, 2):
-                cols = slice(P * t, P * (t + 1))
-                nc.tensor.matmul_mx(
-                    out=y[t][:],
-                    lhsT=w_codes[z][:, cols].bitcast(FP8X4),
-                    lhsT_scale=w_scale[z][:, cols],
-                    rhs=x_codes[:].bitcast(FP8X4),
-                    rhs_scale=x_scale[:, z, :],
-                    start=(z == 0),
-                    stop=(z == PASSES - 1),
-                )
+            pieces = halves if z == PASSES - 1 else [slice(0, S)]
+            for piece in pieces:
+                entries = offs_sb[:, piece.start // 16 : piece.stop // 16]
+                nc.vector.tensor_copy(x_codes[z][:, piece], x_table[z][:].indirect(entries))
+            for h in range(2):
+                multiply(0, y_first[h], halves[h], z)
+            multiply(3, y[3], slice(0, S), z)
 
-        minus_all = keep.tile([P, 2 * S + HELD], F32, name="minus_all")
-        minus_pair = minus_all[:, HELD:]
-        minus_first = keep.tile([P, S], F32, name="minus_first")
-        minus_y = [minus_first[:], minus_all[:, :S], minus_pair[:, S:], minus_pair[:, :S]]
+        minus_all = keep.tile([P, 3 * S], F32, name="minus_all")
+        steps = keep.tile([P, 3 * S], F32, name="steps")
+        place_of = {1: slice(0, S), 3: slice(S, 2 * S), 2: slice(2 * S, 3 * S)}
+        minus_first = minus_all[:, place_of[1]]
+        first_step = minus_all[:, place_of[2]]
 
         def turn_sign(t):
-            nc.scalar.activation(out=minus_y[t], in_=y[t][:], func=ACT.Copy, scale=-1.0)
+            nc.scalar.activation(out=minus_all[:, place_of[t]], in_=y[t][:], func=ACT.Copy, scale=-1.0)
 
-        for t in (0, 3):
-            turn_sign(t)
-        steps = keep.tile([P, 2 * S], F32, name="steps")
-        second_step = keep.tile([P, S], F32, name="second_step")
+        def clip(out, in_):
+            nc.gpsimd.tensor_scalar(out, in_, 0.75, -0.75, ALU.min, ALU.max)
 
-        def clip(engine, out, in_):
-            engine.tensor_scalar(out, in_, 0.75, -0.75, ALU.min, ALU.max)
-
-        clip(nc.gpsimd, minus_y[2], minus_y[0])
-        clip(nc.gpsimd, steps[:, : S - HELD], minus_pair[:, : S - HELD])
+        for h in range(2):
+            nc.scalar.activation(out=minus_first[:, halves[h]], in_=y_first[h][:], func=ACT.Copy, scale=-1.0)
+        for t in (1, 2):
+            multiply_late(t)
+        turn_sign(3)
+        for h in range(2):
+            clip(first_step[:, halves[h]], minus_first[:, halves[h]])
         turn_sign(1)
-        clip(nc.gpsimd, second_step[:], minus_y[1])
+        clip(steps[:, : S + HELD], minus_all[:, : S + HELD])
 
         grouped = [
             keep.tile([P, CHUNK, PACK], BF16, name=f"grouped{c}", align_bytes=64) for c in range(CHUNKS)
@@ -147,7 +167,7 @@ def tile_picked_clipsgd_none_po_kernel(
         decayed = [keep.tile([P, S], F32, name=f"decayed{t}", tag=f"decayed{t}") for t in range(PACK)]
         for t in (0, 1, 2, 3):
             nc.vector.tensor_scalar(decayed[t][:], rows[t][:].indirect(ent_sb[:]), 0.875, 0.0, ALU.mult, ALU.add)
-        step = [minus_y[2], second_step[:], steps[:, S:], steps[:, :S]]
+        step = [first_step] + [steps[:, place_of[t]] for t in range(1, PACK)]
         out_rows = out_0.rearrange("(p t) c -> t p c", t=PACK)
         for t in range(PACK):
             nc.vector.tensor_tensor(rows[t][:].indirect(ent_sb[:]), decayed[t][:], step[t], ALU.add)
@@ -168,7 +188,7 @@ def tile_picked_clipsgd_none_po_kernel(
                     nc.scalar.copy(out=grouped[c][:, :, t], in_=part)
                 if t == 0 and c == 0:
                     turn_sign(2)
-                    clip(nc.gpsimd, steps[:, S - HELD :], minus_pair[:, S - HELD :])
+                    clip(steps[:, S + HELD :], minus_all[:, S + HELD :])
 
         last = PACK - 1
         nc.vector.tensor_copy(out=grouped[0][:, :FILL, last - 1], in_=rows[last - 1][:, :FILL])

@@ -24,6 +24,8 @@ VECTOR_CHUNKS = 2
 EDGE = 8
 FILL = 160
 HELD = 256
+CUTS = (0, 256, 384, 512, 768, 1024)
+STORE_AT = (384, 768, 1024)
 W_BYTES = 4 * PACK * N
 
 
@@ -202,16 +204,17 @@ def tile_picked_clipsgd_none_po_kernel(
         out_codes = keep.tile([P, U], U32, name="out_codes", align_bytes=64)
         out_scale = keep.tile([P, U], U8, name="out_scale", align_bytes=64)
         out_words = out_1[0].rearrange("p c r -> p (c r)").bitcast(I32)
-        for c in range(CHUNKS):
-            cols = slice(c * CHUNK, (c + 1) * CHUNK)
+        stored = 0
+        for first, stop in zip(CUTS, CUTS[1:]):
+            c = first // CHUNK
             nc.vector.quantize_mx(
-                out=out_codes[:, cols].bitcast(FP8X4),
-                scales=out_scale[:, cols],
-                in_=grouped[c][:].rearrange("p c t -> p (c t)"),
+                out=out_codes[:, first:stop].bitcast(FP8X4),
+                scales=out_scale[:, first:stop],
+                in_=grouped[c][:, first - c * CHUNK : stop - c * CHUNK, :].rearrange("p c t -> p (c t)"),
             )
-            if c >= VECTOR_CHUNKS - 1:
-                done = slice(0 if c < VECTOR_CHUNKS else c * CHUNK, (c + 1) * CHUNK)
-                nc.sync.dma_start(out=out_words[:, done], in_=out_codes[:, done].bitcast(I32))
+            if stop in STORE_AT:
+                nc.sync.dma_start(out=out_words[:, stored:stop], in_=out_codes[:, stored:stop].bitcast(I32))
+                stored = stop
         for q in range(4):
             queue = nc.scalar if q % 2 else nc.sync
             queue.dma_start(

@@ -21,8 +21,7 @@ PASSES = K // (P * PACK)
 CHUNK = 256
 CHUNKS = U // CHUNK
 VECTOR_CHUNKS = 2
-EDGE = 8
-FILL = 160
+ORDER = (2, 0, 1, 3)
 HELD = 256
 CUTS = (0, 256, 384, 512, 768, 1024)
 STORE_AT = (384, 768, 1024)
@@ -106,7 +105,7 @@ def tile_picked_clipsgd_none_po_kernel(
         par_rows = par.rearrange("(p t) c -> t p c", t=PACK)
         for place, t in enumerate((0, 1, 2, 3)):
             rows[t] = early.tile([P, U], F32, name=f"rows{t}", offset=place * 4 * U)
-            nc.sync.dma_start(out=rows[t][:], in_=par_rows[t])
+            nc.sync.dma_start(out=rows[t][:], in_=par_rows[ORDER[t]])
             if t == 0:
                 move_last_quadrant(1)
 
@@ -116,7 +115,7 @@ def tile_picked_clipsgd_none_po_kernel(
         x_codes = [keep.tile([P, S], U32, name=f"x_codes{z}", align_bytes=64) for z in range(PASSES)]
 
         def multiply(t, bank, picked, z):
-            cols = slice(P * t, P * (t + 1))
+            cols = slice(P * ORDER[t], P * (ORDER[t] + 1))
             nc.tensor.matmul_mx(
                 out=bank[:],
                 lhsT=w_codes[z][:, cols].bitcast(FP8X4),
@@ -173,27 +172,17 @@ def tile_picked_clipsgd_none_po_kernel(
         out_rows = out_0.rearrange("(p t) c -> t p c", t=PACK)
         for t in range(PACK):
             nc.vector.tensor_tensor(rows[t][:].indirect(ent_sb[:]), decayed[t][:], step[t], ALU.add)
-            nc.sync.dma_start(out=out_rows[t], in_=rows[t][:])
+            nc.sync.dma_start(out=out_rows[ORDER[t]], in_=rows[t][:])
             if t == PACK - 1:
                 break
             for c in range(CHUNKS):
                 part = rows[t][:, c * CHUNK : (c + 1) * CHUNK]
-                if t == PACK - 2 and c < VECTOR_CHUNKS:
-                    first = FILL if c == 0 else 0
-                    edge = CHUNK - EDGE
-                    nc.scalar.copy(out=grouped[c][:, first:edge, t], in_=part[:, first:edge])
-                    nc.scalar.copy(
-                        out=grouped[c][:, edge:, t : t + 2],
-                        in_=part[:, edge:].unsqueeze(2).to_broadcast([P, EDGE, 2]),
-                    )
-                else:
-                    nc.scalar.copy(out=grouped[c][:, :, t], in_=part)
-                if t == 0 and c == 0:
+                nc.scalar.copy(out=grouped[c][:, :, ORDER[t]], in_=part)
+                if t == 0 and c == VECTOR_CHUNKS - 1:
                     turn_sign(2)
                     clip(steps[:, S + HELD :], minus_all[:, S + HELD :])
 
         last = PACK - 1
-        nc.vector.tensor_copy(out=grouped[0][:, :FILL, last - 1], in_=rows[last - 1][:, :FILL])
         for c in range(CHUNKS):
             part = rows[last][:, c * CHUNK : (c + 1) * CHUNK]
             if c < VECTOR_CHUNKS:

@@ -22,10 +22,12 @@ CHUNK = 256
 CHUNKS = U // CHUNK
 VECTOR_CHUNKS = 2
 ORDER = (2, 0, 1, 3)
-HELD = 256
 CUTS = (0, 256, 384, 512, 768, 1024)
 STORE_AT = (384, 768, 1024)
 W_BYTES = 4 * PACK * N
+RAW_AT = {"01": 8192, "1": 14336, "2": 1024, "3": 12288}
+CLIPPED_AT = {"00": 14336, "01": 20480, "1": 16384, "2": 18432, "3": 5120}
+GROUPED_AT = (0, 2048, 4096, 6144)
 
 
 def tile_picked_clipsgd_none_po_kernel(
@@ -66,18 +68,11 @@ def tile_picked_clipsgd_none_po_kernel(
         nc.sync.dma_start(ent_sb[:], ent)
         nc.vector.tensor_copy(x_picked_scale[:], x_scale_table[:].indirect(offs_sb[:]))
 
-        def move_last_quadrant(z):
-            nc.sync.dma_start(
-                out=x_scale[96:100, z, :].bitcast(I32),
-                in_=x_picked_scale[96 + 4 * z : 128 : 8].bitcast(I32),
-            )
-
-        for q in range(3):
+        for q in range(4):
             nc.sync.dma_start(
                 out=x_scale[32 * q : 32 * q + 4].bitcast(I32),
                 in_=x_picked_scale[32 * q : 32 * q + 32 : 4].bitcast(I32),
             )
-        move_last_quadrant(0)
         x_last = early.tile([P, T], U32, name="x_table1", offset=PASSES * W_BYTES)
         load_x(x_last, 1)
         x_table = [x_first, x_last]
@@ -106,12 +101,9 @@ def tile_picked_clipsgd_none_po_kernel(
         for place, t in enumerate((0, 1, 2, 3)):
             rows[t] = early.tile([P, U], F32, name=f"rows{t}", offset=place * 4 * U)
             nc.sync.dma_start(out=rows[t][:], in_=par_rows[ORDER[t]])
-            if t == 0:
-                move_last_quadrant(1)
 
         halves = [slice(0, S // 2), slice(S // 2, S)]
-        y_first = [psum.tile([P, S // 2], F32, name=f"y_first{h}", tag=f"bank{h}") for h in range(2)]
-        y = {3: psum.tile([P, S], F32, name="y3")}
+        whole = slice(0, S)
         x_codes = [keep.tile([P, S], U32, name=f"x_codes{z}", align_bytes=64) for z in range(PASSES)]
 
         def multiply(t, bank, picked, z):
@@ -126,69 +118,82 @@ def tile_picked_clipsgd_none_po_kernel(
                 stop=(z == PASSES - 1),
             )
 
-        def multiply_late(t):
-            y[t] = psum.tile([P, S], F32, name=f"y{t}", tag=f"bank{t - 1}")
+        def product(t, piece, name, tag):
+            bank = psum.tile([P, piece.stop - piece.start], F32, name=f"y{name}", tag=tag)
             for z in range(PASSES):
-                multiply(t, y[t], slice(0, S), z)
+                multiply(t, bank, piece, z)
+            return bank
 
         for z in range(PASSES):
-            pieces = halves if z == PASSES - 1 else [slice(0, S)]
+            pieces = halves if z == PASSES - 1 else [whole]
             for piece in pieces:
                 entries = offs_sb[:, piece.start // 16 : piece.stop // 16]
                 nc.vector.tensor_copy(x_codes[z][:, piece], x_table[z][:].indirect(entries))
-            for h in range(2):
-                multiply(0, y_first[h], halves[h], z)
-            multiply(3, y[3], slice(0, S), z)
 
-        minus_all = keep.tile([P, 3 * S], F32, name="minus_all")
-        steps = keep.tile([P, 3 * S], F32, name="steps")
-        place_of = {1: slice(0, S), 3: slice(S, 2 * S), 2: slice(2 * S, 3 * S)}
-        minus_first = minus_all[:, place_of[1]]
-        first_step = minus_all[:, place_of[2]]
-
-        def turn_sign(t):
-            nc.scalar.activation(out=minus_all[:, place_of[t]], in_=y[t][:], func=ACT.Copy, scale=-1.0)
-
-        def clip(out, in_):
-            nc.gpsimd.tensor_scalar(out, in_, 0.75, -0.75, ALU.min, ALU.max)
-
-        for h in range(2):
-            nc.scalar.activation(out=minus_first[:, halves[h]], in_=y_first[h][:], func=ACT.Copy, scale=-1.0)
-        for t in (1, 2):
-            multiply_late(t)
-        turn_sign(3)
-        for h in range(2):
-            clip(first_step[:, halves[h]], minus_first[:, halves[h]])
-        turn_sign(1)
-        clip(steps[:, : S + HELD], minus_all[:, : S + HELD])
-
-        grouped = [
-            keep.tile([P, CHUNK, PACK], BF16, name=f"grouped{c}", align_bytes=64) for c in range(CHUNKS)
-        ]
-        decayed = [keep.tile([P, S], F32, name=f"decayed{t}", tag=f"decayed{t}") for t in range(PACK)]
-        for t in (0, 1, 2, 3):
-            nc.vector.tensor_scalar(decayed[t][:], rows[t][:].indirect(ent_sb[:]), 0.875, 0.0, ALU.mult, ALU.add)
-        step = [first_step] + [steps[:, place_of[t]] for t in range(1, PACK)]
+        grouped = []
+        held = ctx.enter_context(tc.tile_pool(name="held", bufs=1))
         out_rows = out_0.rearrange("(p t) c -> t p c", t=PACK)
-        for t in range(PACK):
-            nc.vector.tensor_tensor(rows[t][:].indirect(ent_sb[:]), decayed[t][:], step[t], ALU.add)
-            nc.sync.dma_start(out=out_rows[ORDER[t]], in_=rows[t][:])
-            if t == PACK - 1:
-                break
-            for c in range(CHUNKS):
-                part = rows[t][:, c * CHUNK : (c + 1) * CHUNK]
-                nc.scalar.copy(out=grouped[c][:, :, ORDER[t]], in_=part)
-                if t == 0 and c == VECTOR_CHUNKS - 1:
-                    turn_sign(2)
-                    clip(steps[:, S + HELD :], minus_all[:, S + HELD :])
+        new = {}
 
-        last = PACK - 1
-        for c in range(CHUNKS):
-            part = rows[last][:, c * CHUNK : (c + 1) * CHUNK]
-            if c < VECTOR_CHUNKS:
-                nc.vector.tensor_copy(out=grouped[c][:, :, last], in_=part)
+        raw = {}
+
+        def prepare(t, piece, name, tag, on_vector=False):
+            bank = product(t, piece, name, tag)
+            width = piece.stop - piece.start
+            entries = ent_sb[:, piece.start // 16 : piece.stop // 16]
+            clipped = held.tile([P, width], F32, name=f"clipped{name}", offset=CLIPPED_AT[name])
+            decayed = keep.tile([P, width], F32, name=f"decayed{name}")
+            new[name] = keep.tile([P, width], F32, name=f"new{name}")
+            nc.scalar.activation(out=decayed[:], in_=rows[t][:].indirect(entries), func=ACT.Copy, scale=0.875)
+            if on_vector:
+                nc.vector.tensor_scalar(clipped[:], bank[:], 0.75, -0.75, ALU.min, ALU.max)
+                nc.vector.tensor_tensor(new[name][:], decayed[:], clipped[:], ALU.subtract)
             else:
-                nc.scalar.copy(out=grouped[c][:, :, last], in_=part)
+                raw[name] = held.tile([P, width], F32, name=f"raw{name}", offset=RAW_AT[name])
+                nc.scalar.copy(out=raw[name][:], in_=bank[:])
+                nc.gpsimd.tensor_scalar(clipped[:], raw[name][:], 0.75, -0.75, ALU.min, ALU.max)
+                nc.gpsimd.tensor_tensor(new[name][:], decayed[:], clipped[:], ALU.subtract)
+
+        def scatter(t, piece, name):
+            entries = ent_sb[:, piece.start // 16 : piece.stop // 16]
+            nc.vector.tensor_copy(rows[t][:].indirect(entries), new[name][:])
+
+        def store(t):
+            nc.sync.dma_start(out=out_rows[ORDER[t]], in_=rows[t][:])
+
+        def cast(t, c, engine):
+            part = rows[t][:, c * CHUNK : (c + 1) * CHUNK]
+            if engine == "scalar":
+                nc.scalar.copy(out=grouped[c][:, :, ORDER[t]], in_=part)
+            elif engine == "vector":
+                nc.vector.tensor_copy(out=grouped[c][:, :, ORDER[t]], in_=part)
+            else:
+                nc.gpsimd.tensor_copy(out=grouped[c][:, :, ORDER[t]], in_=part)
+
+        prepare(0, halves[0], "00", "bank0", on_vector=True)
+        prepare(0, halves[1], "01", "bank0")
+        for h in range(2):
+            scatter(0, halves[h], f"0{h}")
+        store(0)
+        prepare(1, whole, "1", "bank1")
+        prepare(2, whole, "2", "bank0")
+        for c in range(CHUNKS):
+            grouped.append(held.tile([P, CHUNK, PACK], BF16, name=f"grouped{c}", offset=GROUPED_AT[c], align_bytes=64))
+        for c in range(VECTOR_CHUNKS):
+            cast(0, c, "scalar")
+        prepare(3, whole, "3", "bank1")
+        for c in range(VECTOR_CHUNKS, CHUNKS):
+            cast(0, c, "scalar")
+        for t in (1, 2):
+            scatter(t, whole, str(t))
+            store(t)
+            for c in range(CHUNKS):
+                cast(t, c, "scalar" if c < VECTOR_CHUNKS else "gpsimd")
+        last = PACK - 1
+        scatter(last, whole, str(last))
+        store(last)
+        for c in range(CHUNKS):
+            cast(last, c, "vector" if c < VECTOR_CHUNKS else "scalar")
 
         out_codes = keep.tile([P, U], U32, name="out_codes", align_bytes=64)
         out_scale = keep.tile([P, U], U8, name="out_scale", align_bytes=64)

@@ -25,8 +25,9 @@ ORDER = (2, 0, 1, 3)
 CUTS = (0, 256, 384, 512, 768, 1024)
 STORE_AT = (384, 768, 1024)
 W_BYTES = 4 * PACK * N
-RAW_AT = {"01": 8192, "1": 14336, "2": 1024, "3": 12288}
-CLIPPED_AT = {"00": 14336, "01": 20480, "1": 16384, "2": 18432, "3": 5120}
+RAW_AT = {"1": 12288, "2": 12288, "3": 26624}
+DECAYED_AT = {"00": 12288, "01": 14336, "1": 25600, "2": 16384, "3": 24576}
+CLIPPED_AT = {"00": 8192, "01": 9216, "1": 1024, "2": 18432, "3": 5120}
 GROUPED_AT = (0, 2048, 4096, 6144)
 
 
@@ -137,22 +138,22 @@ def tile_picked_clipsgd_none_po_kernel(
 
         raw = {}
 
-        def prepare(t, piece, name, tag, on_vector=False):
+        def prepare(t, piece, name, tag, on_vector=0):
             bank = product(t, piece, name, tag)
             width = piece.stop - piece.start
             entries = ent_sb[:, piece.start // 16 : piece.stop // 16]
             clipped = held.tile([P, width], F32, name=f"clipped{name}", offset=CLIPPED_AT[name])
-            decayed = keep.tile([P, width], F32, name=f"decayed{name}")
+            decayed = held.tile([P, width], F32, name=f"decayed{name}", offset=DECAYED_AT[name])
             new[name] = keep.tile([P, width], F32, name=f"new{name}")
             nc.scalar.activation(out=decayed[:], in_=rows[t][:].indirect(entries), func=ACT.Copy, scale=0.875)
             if on_vector:
                 nc.vector.tensor_scalar(clipped[:], bank[:], 0.75, -0.75, ALU.min, ALU.max)
-                nc.vector.tensor_tensor(new[name][:], decayed[:], clipped[:], ALU.subtract)
             else:
                 raw[name] = held.tile([P, width], F32, name=f"raw{name}", offset=RAW_AT[name])
                 nc.scalar.copy(out=raw[name][:], in_=bank[:])
                 nc.gpsimd.tensor_scalar(clipped[:], raw[name][:], 0.75, -0.75, ALU.min, ALU.max)
-                nc.gpsimd.tensor_tensor(new[name][:], decayed[:], clipped[:], ALU.subtract)
+            engine = nc.vector if on_vector == 2 else nc.gpsimd
+            engine.tensor_tensor(new[name][:], decayed[:], clipped[:], ALU.subtract)
 
         def scatter(t, piece, name):
             entries = ent_sb[:, piece.start // 16 : piece.stop // 16]
@@ -168,14 +169,14 @@ def tile_picked_clipsgd_none_po_kernel(
             elif engine == "vector":
                 nc.vector.tensor_copy(out=grouped[c][:, :, ORDER[t]], in_=part)
             else:
-                nc.gpsimd.tensor_copy(out=grouped[c][:, :, ORDER[t]], in_=part)
+                nc.gpsimd.tensor_scalar(grouped[c][:, :, ORDER[t]], part, 1.0, 1.0, ALU.mult, ALU.mult)
 
-        prepare(0, halves[0], "00", "bank0", on_vector=True)
-        prepare(0, halves[1], "01", "bank0")
+        prepare(0, halves[0], "00", "bank0", on_vector=2)
+        prepare(0, halves[1], "01", "bank1", on_vector=1)
         for h in range(2):
             scatter(0, halves[h], f"0{h}")
         store(0)
-        prepare(1, whole, "1", "bank1")
+        prepare(1, whole, "1", "bank2")
         prepare(2, whole, "2", "bank0")
         for c in range(CHUNKS):
             grouped.append(held.tile([P, CHUNK, PACK], BF16, name=f"grouped{c}", offset=GROUPED_AT[c], align_bytes=64))

@@ -25,9 +25,14 @@ ORDER = (2, 0, 1, 3)
 CUTS = (0, 256, 384, 512, 768, 1024)
 STORE_AT = (384, 768, 1024)
 W_BYTES = 4 * PACK * N
-RAW_AT = {"1": 12288, "2": 12288, "3": 26624}
-DECAYED_AT = {"00": 12288, "01": 14336, "1": 25600, "2": 16384, "3": 24576}
-CLIPPED_AT = {"00": 8192, "01": 9216, "1": 1024, "2": 18432, "3": 5120}
+PLACE = {
+    "decayed00": 12288, "raw1": 12288, "raw2": 12288,
+    "new00": 34816, "clipped2": 1024,
+    "decayed2": 5120, "new3": 8192,
+    "decayed1": 24576, "decayed3": 26624, "raw3": 28672, "clipped3": 30720, "clipped1": 32768,
+    "clipped00": 10240, "clipped01": 11264, "decayed01": 16384,
+    "new01": 15360, "new1": 20480, "new2": 22528,
+}
 GROUPED_AT = (0, 2048, 4096, 6144)
 
 
@@ -136,24 +141,29 @@ def tile_picked_clipsgd_none_po_kernel(
         out_rows = out_0.rearrange("(p t) c -> t p c", t=PACK)
         new = {}
 
-        raw = {}
+        clipped = {}
 
-        def prepare(t, piece, name, tag, on_vector=0):
+        def buffer(kind, name, width):
+            return held.tile([P, width], F32, name=f"{kind}{name}", offset=PLACE[kind + name])
+
+        def clip(t, piece, name, tag, on_vector=False):
             bank = product(t, piece, name, tag)
             width = piece.stop - piece.start
-            entries = ent_sb[:, piece.start // 16 : piece.stop // 16]
-            clipped = held.tile([P, width], F32, name=f"clipped{name}", offset=CLIPPED_AT[name])
-            decayed = held.tile([P, width], F32, name=f"decayed{name}", offset=DECAYED_AT[name])
-            new[name] = keep.tile([P, width], F32, name=f"new{name}")
-            nc.scalar.activation(out=decayed[:], in_=rows[t][:].indirect(entries), func=ACT.Copy, scale=0.875)
+            clipped[name] = buffer("clipped", name, width)
             if on_vector:
-                nc.vector.tensor_scalar(clipped[:], bank[:], 0.75, -0.75, ALU.min, ALU.max)
+                nc.vector.tensor_scalar(clipped[name][:], bank[:], 0.75, -0.75, ALU.min, ALU.max)
             else:
-                raw[name] = held.tile([P, width], F32, name=f"raw{name}", offset=RAW_AT[name])
-                nc.scalar.copy(out=raw[name][:], in_=bank[:])
-                nc.gpsimd.tensor_scalar(clipped[:], raw[name][:], 0.75, -0.75, ALU.min, ALU.max)
-            engine = nc.vector if on_vector == 2 else nc.gpsimd
-            engine.tensor_tensor(new[name][:], decayed[:], clipped[:], ALU.subtract)
+                raw = buffer("raw", name, width)
+                nc.scalar.copy(out=raw[:], in_=bank[:])
+                nc.gpsimd.tensor_scalar(clipped[name][:], raw[:], 0.75, -0.75, ALU.min, ALU.max)
+
+        def step(t, piece, name, engine):
+            width = piece.stop - piece.start
+            decayed = buffer("decayed", name, 2 * width if name == "2" else width)[:, :width]
+            new[name] = buffer("new", name, width)
+            entries = ent_sb[:, piece.start // 16 : piece.stop // 16]
+            nc.scalar.activation(out=decayed, in_=rows[t][:].indirect(entries), func=ACT.Copy, scale=0.875)
+            engine.tensor_tensor(new[name][:], decayed, clipped[name][:], ALU.subtract)
 
         def scatter(t, piece, name):
             entries = ent_sb[:, piece.start // 16 : piece.stop // 16]
@@ -171,18 +181,22 @@ def tile_picked_clipsgd_none_po_kernel(
             else:
                 nc.gpsimd.tensor_scalar(grouped[c][:, :, ORDER[t]], part, 1.0, 1.0, ALU.mult, ALU.mult)
 
-        prepare(0, halves[0], "00", "bank0", on_vector=2)
-        prepare(0, halves[1], "01", "bank1", on_vector=1)
         for h in range(2):
-            scatter(0, halves[h], f"0{h}")
+            clip(0, halves[h], f"0{h}", f"bank{h}", on_vector=True)
+            step(0, halves[h], f"0{h}", nc.gpsimd if h else nc.vector)
+        scatter(0, halves[0], "00")
+        clip(1, whole, "1", "bank2")
+        step(1, whole, "1", nc.gpsimd)
+        scatter(0, halves[1], "01")
         store(0)
-        prepare(1, whole, "1", "bank2")
-        prepare(2, whole, "2", "bank0")
+        clip(2, whole, "2", "bank0")
+        step(2, whole, "2", nc.gpsimd)
+        clip(3, whole, "3", "bank1")
         for c in range(CHUNKS):
             grouped.append(held.tile([P, CHUNK, PACK], BF16, name=f"grouped{c}", offset=GROUPED_AT[c], align_bytes=64))
         for c in range(VECTOR_CHUNKS):
-            cast(0, c, "scalar")
-        prepare(3, whole, "3", "bank1")
+            cast(0, c, "gpsimd")
+        step(3, whole, "3", nc.gpsimd)
         for c in range(VECTOR_CHUNKS, CHUNKS):
             cast(0, c, "scalar")
         for t in (1, 2):

@@ -26,12 +26,12 @@ CUTS = (0, 256, 384, 512, 768, 1024)
 STORE_AT = (384, 768, 1024)
 W_BYTES = 4 * PACK * N
 PLACE = {
-    "decayed00": 12288, "raw1": 12288, "raw2": 12288,
-    "new00": 34816, "clipped2": 1024,
+    "decayed00": 36864, "clipped10": 12288, "raw11": 12288, "raw2": 12288, "raw3": 12288,
+    "clipped2": 1024,
     "decayed2": 5120, "new3": 8192,
-    "decayed1": 24576, "decayed3": 26624, "raw3": 28672, "clipped3": 30720, "clipped1": 32768,
-    "clipped00": 10240, "clipped01": 11264, "decayed01": 16384,
-    "new01": 15360, "new1": 20480, "new2": 22528,
+    "decayed10": 24576, "decayed11": 25600, "decayed3": 26624, "clipped3": 30720,
+    "clipped00": 10240, "clipped01": 11264, "clipped11": 33792, "decayed01": 16384,
+    "new00": 34816, "new01": 24576, "new10": 20480, "new11": 21504, "new2": 22528,
 }
 GROUPED_AT = (0, 2048, 4096, 6144)
 
@@ -157,13 +157,21 @@ def tile_picked_clipsgd_none_po_kernel(
                 nc.scalar.copy(out=raw[:], in_=bank[:])
                 nc.gpsimd.tensor_scalar(clipped[name][:], raw[:], 0.75, -0.75, ALU.min, ALU.max)
 
-        def step(t, piece, name, engine):
+        decayed = {}
+
+        def fetch(t, piece, name):
             width = piece.stop - piece.start
-            decayed = buffer("decayed", name, 2 * width if name == "2" else width)[:, :width]
-            new[name] = buffer("new", name, width)
+            decayed[name] = buffer("decayed", name, 2 * width if name == "2" else width)[:, :width]
             entries = ent_sb[:, piece.start // 16 : piece.stop // 16]
-            nc.scalar.activation(out=decayed, in_=rows[t][:].indirect(entries), func=ACT.Copy, scale=0.875)
-            engine.tensor_tensor(new[name][:], decayed, clipped[name][:], ALU.subtract)
+            nc.scalar.activation(out=decayed[name], in_=rows[t][:].indirect(entries), func=ACT.Copy, scale=0.875)
+
+        def subtract(name, engine):
+            new[name] = buffer("new", name, decayed[name].shape[1])
+            engine.tensor_tensor(new[name][:], decayed[name], clipped[name][:], ALU.subtract)
+
+        def step(t, piece, name, engine):
+            fetch(t, piece, name)
+            subtract(name, engine)
 
         def scatter(t, piece, name):
             entries = ent_sb[:, piece.start // 16 : piece.stop // 16]
@@ -181,14 +189,24 @@ def tile_picked_clipsgd_none_po_kernel(
             else:
                 nc.gpsimd.tensor_scalar(grouped[c][:, :, ORDER[t]], part, 1.0, 1.0, ALU.mult, ALU.mult)
 
+        clip(0, halves[0], "00", "bank0", on_vector=True)
+        clip(1, halves[0], "10", "bank1", on_vector=True)
         for h in range(2):
-            clip(0, halves[h], f"0{h}", f"bank{h}", on_vector=True)
-            step(0, halves[h], f"0{h}", nc.gpsimd if h else nc.vector)
+            fetch(0, halves[h], f"0{h}")
+        subtract("00", nc.gpsimd)
+        clip(0, halves[1], "01", "bank2", on_vector=True)
         scatter(0, halves[0], "00")
-        clip(1, whole, "1", "bank2")
-        step(1, whole, "1", nc.gpsimd)
+        for h in range(2):
+            fetch(1, halves[h], f"1{h}")
+        subtract("10", nc.gpsimd)
+        subtract("01", nc.gpsimd)
+        clip(1, halves[1], "11", "bank3")
+        subtract("11", nc.gpsimd)
+        scatter(1, halves[0], "10")
         scatter(0, halves[1], "01")
         store(0)
+        scatter(1, halves[1], "11")
+        store(1)
         clip(2, whole, "2", "bank0")
         step(2, whole, "2", nc.gpsimd)
         clip(3, whole, "3", "bank1")
@@ -200,8 +218,9 @@ def tile_picked_clipsgd_none_po_kernel(
         for c in range(VECTOR_CHUNKS, CHUNKS):
             cast(0, c, "scalar")
         for t in (1, 2):
-            scatter(t, whole, str(t))
-            store(t)
+            if t == 2:
+                scatter(t, whole, str(t))
+                store(t)
             for c in range(CHUNKS):
                 cast(t, c, "scalar" if c < VECTOR_CHUNKS else "gpsimd")
         last = PACK - 1

@@ -222,7 +222,7 @@ def tile_picked_clipsgd_none_po_kernel(
                 scatter(t, whole, str(t))
                 store(t)
             for c in range(CHUNKS):
-                cast(t, c, "scalar" if c < VECTOR_CHUNKS else "gpsimd")
+                cast(t, c, "scalar" if c < CHUNKS - 1 else "gpsimd")
         last = PACK - 1
         scatter(last, whole, str(last))
         store(last)

@@ -15,25 +15,36 @@ FP8X4 = mybir.dt.float8_e4m3fn_x4
 ALU = mybir.AluOpType
 ACT = mybir.ActivationFunctionType
 
+DECAY = 0.875
+LIMIT = 0.75
+
 P = 128
 PACK = 4
 PASSES = K // (P * PACK)
+QUADRANTS = 4
+LIST_ROWS = 16
+W_BYTES = 4 * PACK * N
+ROW_BYTES = 4 * U
+
+SLOT = (2, 0, 1, 3)
+LAST = PACK - 1
+
 CHUNK = 256
 CHUNKS = U // CHUNK
 VECTOR_CHUNKS = 2
-ORDER = (2, 0, 1, 3)
 CUTS = (0, 256, 384, 512, 768, 1024)
 STORE_AT = (384, 768, 1024)
-W_BYTES = 4 * PACK * N
-PLACE = {
-    "decayed00": 36864, "clipped10": 12288, "raw11": 12288, "raw2": 12288, "raw3": 12288,
-    "clipped2": 1024,
-    "decayed2": 5120, "new3": 8192,
-    "decayed10": 24576, "decayed11": 25600, "decayed3": 26624, "clipped3": 30720,
-    "clipped00": 10240, "clipped01": 11264, "clipped11": 33792, "decayed01": 16384,
-    "new00": 34816, "new01": 24576, "new10": 20480, "new11": 21504, "new2": 22528,
-}
-GROUPED_AT = (0, 2048, 4096, 6144)
+
+HALF_BYTES = 4 * S // 2
+WHOLE_BYTES = 4 * S
+CHUNK_BYTES = 2 * PACK * CHUNK
+AFTER_CHUNKS = 3 * CHUNK_BYTES
+STAGE_AT = AFTER_CHUNKS + WHOLE_BYTES
+CLIPPED_2_AT = CHUNK_BYTES - HALF_BYTES
+DECAYED_2_AT = AFTER_CHUNKS - HALF_BYTES
+NEW_3_AT = AFTER_CHUNKS
+CHUNK_AT = (0, CHUNK_BYTES, 2 * CHUNK_BYTES, STAGE_AT)
+HANDED_ON_AT = STAGE_AT + WHOLE_BYTES
 
 
 def tile_picked_clipsgd_none_po_kernel(
@@ -43,15 +54,19 @@ def tile_picked_clipsgd_none_po_kernel(
     with ExitStack() as ctx:
         keep = ctx.enter_context(tc.tile_pool(name="keep", bufs=1))
         psum = ctx.enter_context(tc.psum_pool(name="psum", bufs=1))
+        loads = ctx.enter_context(tc.tile_pool(name="loads", bufs=1))
+        reused = ctx.enter_context(tc.tile_pool(name="reused", bufs=1))
 
-        offs_sb = keep.tile([P, S // 16], U16, name="offs_sb")
-        ent_sb = keep.tile([P, S // 16], U16, name="ent_sb")
-        early = ctx.enter_context(tc.tile_pool(name="early", bufs=1))
-        w_raw = [early.tile([P, PACK, N], F32, name=f"w_raw{z}", offset=z * W_BYTES) for z in range(PASSES)]
-        x_scale_table = early.tile([P, T], U8, name="x_scale_table", offset=PASSES * W_BYTES)
+        offs_sb = keep.tile([P, S // LIST_ROWS], U16, name="offs_sb")
+        ent_sb = keep.tile([P, S // LIST_ROWS], U16, name="ent_sb")
+        w_raw = [loads.tile([P, PACK, N], F32, name=f"w_raw{z}", offset=z * W_BYTES) for z in range(PASSES)]
+        x_scale_table = loads.tile([P, T], U8, name="x_scale_table", offset=PASSES * W_BYTES)
         x_first = keep.tile([P, T], U32, name="x_table0", align_bytes=64)
         x_picked_scale = keep.tile([P, S], U8, name="x_picked_scale", align_bytes=64)
         x_scale = keep.tile([P, PASSES, S], U8, name="x_scale", align_bytes=64)
+
+        def entries(list_sb, piece):
+            return list_sb[:, piece.start // LIST_ROWS : piece.stop // LIST_ROWS]
 
         def load_x(table, z):
             nc.sync.dma_start(
@@ -61,33 +76,34 @@ def tile_picked_clipsgd_none_po_kernel(
 
         nc.vector.memset(x_scale_table[:].bitcast(I32), 0)
         nc.vector.memset(x_scale[:].rearrange("p z c -> p (z c)").bitcast(I32), 0)
+
         w_passes = w1.rearrange("(z p j) c -> z p j c", z=PASSES, j=PACK)
-        nc.sync.dma_start(out=w_raw[0][:, :2, :], in_=w_passes[0][:, :2, :])
+        nc.sync.dma_start(out=w_raw[0][:, : PACK // 2, :], in_=w_passes[0][:, : PACK // 2, :])
         nc.sync.dma_start(
-            out=x_scale_table[0:128:4].bitcast(I32),
+            out=x_scale_table[0:P:4].bitcast(I32),
             in_=x_scales.rearrange("z q c -> q z c").bitcast(I32),
         )
         nc.sync.dma_start(offs_sb[:], offs)
-        nc.sync.dma_start(out=w_raw[0][:, 2:, :], in_=w_passes[0][:, 2:, :])
+        nc.sync.dma_start(out=w_raw[0][:, PACK // 2 :, :], in_=w_passes[0][:, PACK // 2 :, :])
         nc.sync.dma_start(out=w_raw[1][:], in_=w_passes[1])
         load_x(x_first, 0)
         nc.sync.dma_start(ent_sb[:], ent)
-        nc.vector.tensor_copy(x_picked_scale[:], x_scale_table[:].indirect(offs_sb[:]))
 
-        for q in range(4):
+        nc.vector.tensor_copy(x_picked_scale[:], x_scale_table[:].indirect(offs_sb[:]))
+        for q in range(QUADRANTS):
             nc.sync.dma_start(
                 out=x_scale[32 * q : 32 * q + 4].bitcast(I32),
                 in_=x_picked_scale[32 * q : 32 * q + 32 : 4].bitcast(I32),
             )
-        x_last = early.tile([P, T], U32, name="x_table1", offset=PASSES * W_BYTES)
+        x_last = loads.tile([P, T], U32, name="x_table1", offset=PASSES * W_BYTES)
         load_x(x_last, 1)
         x_table = [x_first, x_last]
 
         w_codes, w_scale = [], []
         for z in range(PASSES):
             w_bf = keep.tile([P, PACK, P, PACK], BF16, name=f"w_bf{z}", align_bytes=64)
-            dealt = w_bf[:].rearrange("p t m j -> p m j t")
-            source = w_raw[z][:].rearrange("p j (m t) -> p m j t", t=PACK)
+            dealt = w_bf[:].rearrange("p s m j -> p m j s")
+            source = w_raw[z][:].rearrange("p j (m s) -> p m j s", s=PACK)
             if z == 1:
                 nc.scalar.copy(out=dealt, in_=source)
             else:
@@ -97,137 +113,143 @@ def tile_picked_clipsgd_none_po_kernel(
             nc.vector.quantize_mx(
                 out=codes[:].bitcast(FP8X4),
                 scales=scale[:],
-                in_=w_bf[:].rearrange("p t m j -> p (t m j)"),
+                in_=w_bf[:].rearrange("p s m j -> p (s m j)"),
             )
             w_codes.append(codes)
             w_scale.append(scale)
 
-        rows = {}
-        par_rows = par.rearrange("(p t) c -> t p c", t=PACK)
-        for place, t in enumerate((0, 1, 2, 3)):
-            rows[t] = early.tile([P, U], F32, name=f"rows{t}", offset=place * 4 * U)
-            nc.sync.dma_start(out=rows[t][:], in_=par_rows[ORDER[t]])
+        par_rows = par.rearrange("(p s) c -> s p c", s=PACK)
+        out_rows = out_0.rearrange("(p s) c -> s p c", s=PACK)
+        rows = []
+        for turn in range(PACK):
+            rows.append(loads.tile([P, U], F32, name=f"rows{turn}", offset=turn * ROW_BYTES))
+            nc.sync.dma_start(out=rows[turn][:], in_=par_rows[SLOT[turn]])
 
-        halves = [slice(0, S // 2), slice(S // 2, S)]
-        whole = slice(0, S)
+        first_half, second_half, whole = slice(0, S // 2), slice(S // 2, S), slice(0, S)
         x_codes = [keep.tile([P, S], U32, name=f"x_codes{z}", align_bytes=64) for z in range(PASSES)]
-
-        def multiply(t, bank, picked, z):
-            cols = slice(P * ORDER[t], P * (ORDER[t] + 1))
-            nc.tensor.matmul_mx(
-                out=bank[:],
-                lhsT=w_codes[z][:, cols].bitcast(FP8X4),
-                lhsT_scale=w_scale[z][:, cols],
-                rhs=x_codes[z][:, picked].bitcast(FP8X4),
-                rhs_scale=x_scale[:, z, picked],
-                start=(z == 0),
-                stop=(z == PASSES - 1),
-            )
-
-        def product(t, piece, name, tag):
-            bank = psum.tile([P, piece.stop - piece.start], F32, name=f"y{name}", tag=tag)
-            for z in range(PASSES):
-                multiply(t, bank, piece, z)
-            return bank
-
         for z in range(PASSES):
-            pieces = halves if z == PASSES - 1 else [whole]
-            for piece in pieces:
-                entries = offs_sb[:, piece.start // 16 : piece.stop // 16]
-                nc.vector.tensor_copy(x_codes[z][:, piece], x_table[z][:].indirect(entries))
+            for piece in (first_half, second_half) if z == PASSES - 1 else (whole,):
+                nc.vector.tensor_copy(x_codes[z][:, piece], x_table[z][:].indirect(entries(offs_sb, piece)))
 
-        grouped = []
-        held = ctx.enter_context(tc.tile_pool(name="held", bufs=1))
-        out_rows = out_0.rearrange("(p t) c -> t p c", t=PACK)
-        new = {}
+        def values(kind, turn, piece, at):
+            shape, name = [P, piece.stop - piece.start], f"{kind}{turn}_{piece.start}"
+            if at is None:
+                return keep.tile(shape, F32, name=name)
+            return reused.tile(shape, F32, name=name, offset=at)
 
-        clipped = {}
+        def product(turn, piece, bank):
+            y = psum.tile([P, piece.stop - piece.start], F32, name=f"y{turn}_{piece.start}", tag=f"bank{bank}")
+            cols = slice(P * SLOT[turn], P * (SLOT[turn] + 1))
+            for z in range(PASSES):
+                nc.tensor.matmul_mx(
+                    out=y[:],
+                    lhsT=w_codes[z][:, cols].bitcast(FP8X4),
+                    lhsT_scale=w_scale[z][:, cols],
+                    rhs=x_codes[z][:, piece].bitcast(FP8X4),
+                    rhs_scale=x_scale[:, z, piece],
+                    start=(z == 0),
+                    stop=(z == PASSES - 1),
+                )
+            return y
 
-        def buffer(kind, name, width):
-            return held.tile([P, width], F32, name=f"{kind}{name}", offset=PLACE[kind + name])
+        def clip_on_vector(turn, piece, bank, at=None):
+            y = product(turn, piece, bank)
+            clipped = values("clipped", turn, piece, at)
+            nc.vector.tensor_scalar(clipped[:], y[:], LIMIT, -LIMIT, ALU.min, ALU.max)
+            return clipped
 
-        def clip(t, piece, name, tag, on_vector=False):
-            bank = product(t, piece, name, tag)
-            width = piece.stop - piece.start
-            clipped[name] = buffer("clipped", name, width)
-            if on_vector:
-                nc.vector.tensor_scalar(clipped[name][:], bank[:], 0.75, -0.75, ALU.min, ALU.max)
-            else:
-                raw = buffer("raw", name, width)
-                nc.scalar.copy(out=raw[:], in_=bank[:])
-                nc.gpsimd.tensor_scalar(clipped[name][:], raw[:], 0.75, -0.75, ALU.min, ALU.max)
+        def clip_on_gpsimd(turn, piece, bank, at=None):
+            y = product(turn, piece, bank)
+            clipped = values("clipped", turn, piece, at)
+            staged = values("staged", turn, piece, STAGE_AT)
+            nc.scalar.copy(out=staged[:], in_=y[:])
+            nc.gpsimd.tensor_scalar(clipped[:], staged[:], LIMIT, -LIMIT, ALU.min, ALU.max)
+            return clipped
 
-        decayed = {}
+        def fetch(turn, piece, at=None):
+            decayed = values("decayed", turn, piece, at)
+            nc.scalar.activation(
+                out=decayed[:], in_=rows[turn][:].indirect(entries(ent_sb, piece)), func=ACT.Copy, scale=DECAY
+            )
+            return decayed
 
-        def fetch(t, piece, name):
-            width = piece.stop - piece.start
-            decayed[name] = buffer("decayed", name, 2 * width if name == "2" else width)[:, :width]
-            entries = ent_sb[:, piece.start // 16 : piece.stop // 16]
-            nc.scalar.activation(out=decayed[name], in_=rows[t][:].indirect(entries), func=ACT.Copy, scale=0.875)
+        def subtract(turn, piece, decayed, clipped, at=None):
+            new = values("new", turn, piece, at)
+            nc.gpsimd.tensor_tensor(new[:], decayed[:], clipped[:], ALU.subtract)
+            return new
 
-        def subtract(name, engine):
-            new[name] = buffer("new", name, decayed[name].shape[1])
-            engine.tensor_tensor(new[name][:], decayed[name], clipped[name][:], ALU.subtract)
+        def scatter(turn, piece, new):
+            nc.vector.tensor_copy(rows[turn][:].indirect(entries(ent_sb, piece)), new[:])
 
-        def step(t, piece, name, engine):
-            fetch(t, piece, name)
-            subtract(name, engine)
+        def store(turn):
+            nc.sync.dma_start(out=out_rows[SLOT[turn]], in_=rows[turn][:])
 
-        def scatter(t, piece, name):
-            entries = ent_sb[:, piece.start // 16 : piece.stop // 16]
-            nc.vector.tensor_copy(rows[t][:].indirect(entries), new[name][:])
-
-        def store(t):
-            nc.sync.dma_start(out=out_rows[ORDER[t]], in_=rows[t][:])
-
-        def cast(t, c, engine):
-            part = rows[t][:, c * CHUNK : (c + 1) * CHUNK]
-            if engine == "scalar":
-                nc.scalar.copy(out=grouped[c][:, :, ORDER[t]], in_=part)
-            elif engine == "vector":
-                nc.vector.tensor_copy(out=grouped[c][:, :, ORDER[t]], in_=part)
-            else:
-                nc.gpsimd.tensor_scalar(grouped[c][:, :, ORDER[t]], part, 1.0, 1.0, ALU.mult, ALU.mult)
-
-        clip(0, halves[0], "00", "bank0", on_vector=True)
-        clip(1, halves[0], "10", "bank1", on_vector=True)
-        for h in range(2):
-            fetch(0, halves[h], f"0{h}")
-        subtract("00", nc.gpsimd)
-        clip(0, halves[1], "01", "bank2", on_vector=True)
-        scatter(0, halves[0], "00")
-        for h in range(2):
-            fetch(1, halves[h], f"1{h}")
-        subtract("10", nc.gpsimd)
-        subtract("01", nc.gpsimd)
-        clip(1, halves[1], "11", "bank3")
-        subtract("11", nc.gpsimd)
-        scatter(1, halves[0], "10")
-        scatter(0, halves[1], "01")
+        clipped_0a = clip_on_vector(0, first_half, 0)
+        clipped_1a = clip_on_vector(1, first_half, 1, at=STAGE_AT)
+        decayed_0a = fetch(0, first_half)
+        decayed_0b = fetch(0, second_half)
+        new_0a = subtract(0, first_half, decayed_0a, clipped_0a)
+        clipped_0b = clip_on_vector(0, second_half, 2)
+        scatter(0, first_half, new_0a)
+        decayed_1a = fetch(1, first_half, at=HANDED_ON_AT)
+        decayed_1b = fetch(1, second_half)
+        new_1a = subtract(1, first_half, decayed_1a, clipped_1a)
+        new_0b = subtract(0, second_half, decayed_0b, clipped_0b, at=HANDED_ON_AT)
+        clipped_1b = clip_on_gpsimd(1, second_half, 3)
+        new_1b = subtract(1, second_half, decayed_1b, clipped_1b)
+        scatter(1, first_half, new_1a)
+        scatter(0, second_half, new_0b)
         store(0)
-        scatter(1, halves[1], "11")
+        scatter(1, second_half, new_1b)
         store(1)
-        clip(2, whole, "2", "bank0")
-        step(2, whole, "2", nc.gpsimd)
-        clip(3, whole, "3", "bank1")
-        for c in range(CHUNKS):
-            grouped.append(held.tile([P, CHUNK, PACK], BF16, name=f"grouped{c}", offset=GROUPED_AT[c], align_bytes=64))
+
+        clipped_2 = clip_on_gpsimd(2, whole, 0, at=CLIPPED_2_AT)
+        decayed_2 = fetch(2, whole, at=DECAYED_2_AT)
+        new_2 = subtract(2, whole, decayed_2, clipped_2)
+        clipped_3 = clip_on_gpsimd(LAST, whole, 1)
+
+        grouped = [
+            reused.tile([P, CHUNK, PACK], BF16, name=f"grouped{c}", offset=CHUNK_AT[c], align_bytes=64)
+            for c in range(CHUNKS)
+        ]
+
+        def rounding(turn, c):
+            return grouped[c][:, :, SLOT[turn]], rows[turn][:, c * CHUNK : (c + 1) * CHUNK]
+
+        def round_on_scalar(turn, c):
+            out, in_ = rounding(turn, c)
+            nc.scalar.copy(out=out, in_=in_)
+
+        def round_on_vector(turn, c):
+            out, in_ = rounding(turn, c)
+            nc.vector.tensor_copy(out=out, in_=in_)
+
+        def round_on_gpsimd(turn, c):
+            out, in_ = rounding(turn, c)
+            nc.gpsimd.tensor_scalar(out, in_, 1.0, 1.0, ALU.mult, ALU.mult)
+
         for c in range(VECTOR_CHUNKS):
-            cast(0, c, "gpsimd")
-        step(3, whole, "3", nc.gpsimd)
+            round_on_gpsimd(0, c)
+        decayed_3 = fetch(LAST, whole)
+        new_3 = subtract(LAST, whole, decayed_3, clipped_3, at=NEW_3_AT)
         for c in range(VECTOR_CHUNKS, CHUNKS):
-            cast(0, c, "scalar")
-        for t in (1, 2):
-            if t == 2:
-                scatter(t, whole, str(t))
-                store(t)
-            for c in range(CHUNKS):
-                cast(t, c, "scalar" if c < CHUNKS - 1 else "gpsimd")
-        last = PACK - 1
-        scatter(last, whole, str(last))
-        store(last)
-        for c in range(CHUNKS):
-            cast(last, c, "vector" if c < VECTOR_CHUNKS else "scalar")
+            round_on_scalar(0, c)
+
+        def round_middle_turn(turn):
+            for c in range(CHUNKS - 1):
+                round_on_scalar(turn, c)
+            round_on_gpsimd(turn, CHUNKS - 1)
+
+        round_middle_turn(1)
+        scatter(2, whole, new_2)
+        store(2)
+        round_middle_turn(2)
+        scatter(LAST, whole, new_3)
+        store(LAST)
+        for c in range(VECTOR_CHUNKS):
+            round_on_vector(LAST, c)
+        for c in range(VECTOR_CHUNKS, CHUNKS):
+            round_on_scalar(LAST, c)
 
         out_codes = keep.tile([P, U], U32, name="out_codes", align_bytes=64)
         out_scale = keep.tile([P, U], U8, name="out_scale", align_bytes=64)
@@ -238,12 +260,12 @@ def tile_picked_clipsgd_none_po_kernel(
             nc.vector.quantize_mx(
                 out=out_codes[:, first:stop].bitcast(FP8X4),
                 scales=out_scale[:, first:stop],
-                in_=grouped[c][:, first - c * CHUNK : stop - c * CHUNK, :].rearrange("p c t -> p (c t)"),
+                in_=grouped[c][:, first - c * CHUNK : stop - c * CHUNK, :].rearrange("p c s -> p (c s)"),
             )
             if stop in STORE_AT:
                 nc.sync.dma_start(out=out_words[:, stored:stop], in_=out_codes[:, stored:stop].bitcast(I32))
                 stored = stop
-        for q in range(4):
+        for q in range(QUADRANTS):
             queue = nc.scalar if q % 2 else nc.sync
             queue.dma_start(
                 out=out_2[0, 4 * q : 4 * q + 4, :].bitcast(I32),

@@ -128,7 +128,7 @@ def tile_picked_clipsgd_none_po_kernel(
         first_half, second_half, whole = slice(0, S // 2), slice(S // 2, S), slice(0, S)
         x_codes = [keep.tile([P, S], U32, name=f"x_codes{z}", align_bytes=64) for z in range(PASSES)]
         for z in range(PASSES):
-            for piece in (first_half, second_half) if z == PASSES - 1 else (whole,):
+            for piece in (first_half, second_half):
                 nc.vector.tensor_copy(x_codes[z][:, piece], x_table[z][:].indirect(entries(offs_sb, piece)))
 
         def values(kind, turn, piece, at):
@@ -203,7 +203,7 @@ def tile_picked_clipsgd_none_po_kernel(
         scatter(1, second_half, new_1b)
         store(1)
 
-        clipped_2 = clip_on_gpsimd(2, whole, 0, at=CLIPPED_2_AT)
+        clipped_2 = clip_on_gpsimd(2, whole, 4, at=CLIPPED_2_AT)
         decayed_2 = fetch(2, whole, at=DECAYED_2_AT)
         new_2 = subtract(2, whole, decayed_2, clipped_2)
         clipped_3 = clip_on_gpsimd(LAST, whole, 1)

@@ -25,26 +25,22 @@ QUADRANTS = 4
 LIST_ROWS = 16
 W_BYTES = 4 * PACK * N
 ROW_BYTES = 4 * U
+TABLE_AT = PASSES * W_BYTES
+ROUNDED_AT = TABLE_AT + 4 * T
 
 SLOT = (2, 0, 1, 3)
 LAST = PACK - 1
-
 CHUNK = 256
 CHUNKS = U // CHUNK
 VECTOR_CHUNKS = 2
 CUTS = (0, 256, 384, 512, 768, 1024)
 STORE_AT = (384, 768, 1024)
 
-HALF_BYTES = 4 * S // 2
-WHOLE_BYTES = 4 * S
+HALF = 4 * S // 2
 CHUNK_BYTES = 2 * PACK * CHUNK
-AFTER_CHUNKS = 3 * CHUNK_BYTES
-STAGE_AT = AFTER_CHUNKS + WHOLE_BYTES
-CLIPPED_2_AT = CHUNK_BYTES - HALF_BYTES
-DECAYED_2_AT = AFTER_CHUNKS - HALF_BYTES
-NEW_3_AT = AFTER_CHUNKS
-CHUNK_AT = (0, CHUNK_BYTES, 2 * CHUNK_BYTES, STAGE_AT)
-HANDED_ON_AT = STAGE_AT + WHOLE_BYTES
+CLIPPED_2_AT = CHUNK_BYTES - HALF
+RAISED_3_AT = 3 * CHUNK_BYTES - 3 * HALF // 2
+HANDED_ON_AT = 4 * CHUNK_BYTES
 
 
 def tile_picked_clipsgd_none_po_kernel(
@@ -60,7 +56,7 @@ def tile_picked_clipsgd_none_po_kernel(
         offs_sb = keep.tile([P, S // LIST_ROWS], U16, name="offs_sb")
         ent_sb = keep.tile([P, S // LIST_ROWS], U16, name="ent_sb")
         w_raw = [loads.tile([P, PACK, N], F32, name=f"w_raw{z}", offset=z * W_BYTES) for z in range(PASSES)]
-        x_scale_table = loads.tile([P, T], U8, name="x_scale_table", offset=PASSES * W_BYTES)
+        x_scale_table = loads.tile([P, T], U8, name="x_scale_table", offset=TABLE_AT)
         x_first = keep.tile([P, T], U32, name="x_table0", align_bytes=64)
         x_picked_scale = keep.tile([P, S], U8, name="x_picked_scale", align_bytes=64)
         x_scale = keep.tile([P, PASSES, S], U8, name="x_scale", align_bytes=64)
@@ -90,24 +86,31 @@ def tile_picked_clipsgd_none_po_kernel(
         nc.sync.dma_start(ent_sb[:], ent)
 
         nc.vector.tensor_copy(x_picked_scale[:], x_scale_table[:].indirect(offs_sb[:]))
-        for q in range(QUADRANTS):
+        first_half, second_half, whole = slice(0, S // 2), slice(S // 2, S), slice(0, S)
+
+        def move_scales(q, piece):
             nc.sync.dma_start(
-                out=x_scale[32 * q : 32 * q + 4].bitcast(I32),
-                in_=x_picked_scale[32 * q : 32 * q + 32 : 4].bitcast(I32),
+                out=x_scale[32 * q : 32 * q + 4, :, piece].bitcast(I32),
+                in_=x_picked_scale[32 * q : 32 * q + 32 : 4, piece].bitcast(I32),
             )
-        x_last = loads.tile([P, T], U32, name="x_table1", offset=PASSES * W_BYTES)
+
+        for q in range(QUADRANTS):
+            move_scales(q, whole if q < QUADRANTS - 1 else first_half)
+        x_last = loads.tile([P, T], U32, name="x_table1", offset=TABLE_AT)
         load_x(x_last, 1)
         x_table = [x_first, x_last]
 
         w_codes, w_scale = [], []
         for z in range(PASSES):
-            w_bf = keep.tile([P, PACK, P, PACK], BF16, name=f"w_bf{z}", align_bytes=64)
+            w_bf = loads.tile(
+                [P, PACK, P, PACK], BF16, name=f"w_bf{z}", align_bytes=64, offset=ROUNDED_AT + z * ROW_BYTES
+            )
             dealt = w_bf[:].rearrange("p s m j -> p m j s")
             source = w_raw[z][:].rearrange("p j (m s) -> p m j s", s=PACK)
             if z == 1:
-                nc.scalar.copy(out=dealt, in_=source)
+                nc.scalar.activation(out=dealt, in_=source, func=ACT.Copy, scale=-1.0)
             else:
-                nc.vector.tensor_copy(out=dealt, in_=source)
+                nc.vector.tensor_scalar(dealt, source, -1.0, None, ALU.mult)
             codes = keep.tile([P, N], U32, name=f"w_codes{z}", align_bytes=64)
             scale = keep.tile([P, N], U8, name=f"w_scale{z}", align_bytes=64)
             nc.vector.quantize_mx(
@@ -124,8 +127,11 @@ def tile_picked_clipsgd_none_po_kernel(
         for turn in range(PACK):
             rows.append(loads.tile([P, U], F32, name=f"rows{turn}", offset=turn * ROW_BYTES))
             nc.sync.dma_start(out=rows[turn][:], in_=par_rows[SLOT[turn]])
+            if turn == 1:
+                move_scales(QUADRANTS - 1, second_half)
+                rows_again = loads.tile([P, U], F32, name="rows_again", offset=ROUNDED_AT)
+                nc.sync.dma_start(out=rows_again[:], in_=par_rows[SLOT[0]])
 
-        first_half, second_half, whole = slice(0, S // 2), slice(S // 2, S), slice(0, S)
         x_codes = [keep.tile([P, S], U32, name=f"x_codes{z}", align_bytes=64) for z in range(PASSES)]
         for z in range(PASSES):
             for piece in (first_half, second_half):
@@ -152,64 +158,76 @@ def tile_picked_clipsgd_none_po_kernel(
                 )
             return y
 
-        def clip_on_vector(turn, piece, bank, at=None):
+        def clip_on_vector(turn, piece, bank):
             y = product(turn, piece, bank)
-            clipped = values("clipped", turn, piece, at)
+            clipped = values("clipped", turn, piece, None)
             nc.vector.tensor_scalar(clipped[:], y[:], LIMIT, -LIMIT, ALU.min, ALU.max)
             return clipped
 
-        def clip_on_gpsimd(turn, piece, bank, at=None):
+        def after_fetch(name, piece, at):
+            return loads.tile([P, piece.stop - piece.start], F32, name=name, offset=ROUNDED_AT + at)
+
+        def clip_below(turn, piece, bank, raised):
             y = product(turn, piece, bank)
-            clipped = values("clipped", turn, piece, at)
-            staged = values("staged", turn, piece, STAGE_AT)
-            nc.scalar.copy(out=staged[:], in_=y[:])
-            nc.gpsimd.tensor_scalar(clipped[:], staged[:], LIMIT, -LIMIT, ALU.min, ALU.max)
+            nc.scalar.activation(out=raised[:], in_=y[:], func=ACT.Relu, scale=-1.0, bias=LIMIT)
+            return raised
+
+        def clip_above(raised, clipped):
+            nc.scalar.activation(out=clipped[:], in_=raised[:], func=ACT.Relu, scale=-1.0, bias=2 * LIMIT)
             return clipped
 
-        def fetch(turn, piece, at=None):
-            decayed = values("decayed", turn, piece, at)
+        def fetch_into(out, piece, window, shift):
             nc.scalar.activation(
-                out=decayed[:], in_=rows[turn][:].indirect(entries(ent_sb, piece)), func=ACT.Copy, scale=DECAY
+                out=out, in_=window[:].indirect(entries(ent_sb, piece)), func=ACT.Copy, scale=DECAY, bias=shift
             )
-            return decayed
 
-        def subtract(turn, piece, decayed, clipped, at=None):
-            new = values("new", turn, piece, at)
-            nc.gpsimd.tensor_tensor(new[:], decayed[:], clipped[:], ALU.subtract)
-            return new
+        def fetch(turn, piece, window, shift):
+            decayed = values("decayed", turn, piece, None)
+            fetch_into(decayed[:], piece, window, shift)
+            return decayed
 
         def scatter(turn, piece, new):
             nc.vector.tensor_copy(rows[turn][:].indirect(entries(ent_sb, piece)), new[:])
+
+        def scatter_sum(turn, piece, decayed, clipped):
+            nc.vector.tensor_tensor(rows[turn][:].indirect(entries(ent_sb, piece)), decayed[:], clipped[:], ALU.add)
 
         def store(turn):
             nc.sync.dma_start(out=out_rows[SLOT[turn]], in_=rows[turn][:])
 
         clipped_0a = clip_on_vector(0, first_half, 0)
-        clipped_1a = clip_on_vector(1, first_half, 1, at=STAGE_AT)
-        decayed_0a = fetch(0, first_half)
-        decayed_0b = fetch(0, second_half)
-        new_0a = subtract(0, first_half, decayed_0a, clipped_0a)
-        clipped_0b = clip_on_vector(0, second_half, 2)
-        scatter(0, first_half, new_0a)
-        decayed_1a = fetch(1, first_half, at=HANDED_ON_AT)
-        decayed_1b = fetch(1, second_half)
-        new_1a = subtract(1, first_half, decayed_1a, clipped_1a)
-        new_0b = subtract(0, second_half, decayed_0b, clipped_0b, at=HANDED_ON_AT)
-        clipped_1b = clip_on_gpsimd(1, second_half, 3)
-        new_1b = subtract(1, second_half, decayed_1b, clipped_1b)
-        scatter(1, first_half, new_1a)
-        scatter(0, second_half, new_0b)
+        clipped_1a = clip_on_vector(1, first_half, 1)
+        decayed_0a = fetch(0, first_half, rows[0], 0.0)
+        scatter_sum(0, first_half, decayed_0a, clipped_0a)
+        decayed_1a = fetch(1, first_half, rows[1], 0.0)
+        decayed_1b = fetch(1, second_half, rows[1], -LIMIT)
+        scatter_sum(1, first_half, decayed_1a, clipped_1a)
+        raised_0b = clip_below(0, second_half, 2, values("raised", 0, second_half, HANDED_ON_AT))
+        decayed_0b = fetch(0, second_half, rows_again, -LIMIT)
+        y_1b = product(1, second_half, 4)
+        capped_1b = values("capped", 1, second_half, None)
+        nc.scalar.activation(out=capped_1b[:], in_=y_1b[:], func=ACT.Relu, bias=LIMIT)
+        clipped_0b = clip_above(raised_0b, after_fetch("clipped_0b", second_half, 0))
+        new_1b = values("new", 1, second_half, HANDED_ON_AT)
+        nc.vector.scalar_tensor_tensor(new_1b[:], capped_1b[:], 2 * LIMIT, decayed_1b[:], ALU.min, ALU.add)
+        scatter_sum(0, second_half, decayed_0b, clipped_0b)
         store(0)
         scatter(1, second_half, new_1b)
         store(1)
 
-        clipped_2 = clip_on_gpsimd(2, whole, 4, at=CLIPPED_2_AT)
-        decayed_2 = fetch(2, whole, at=DECAYED_2_AT)
-        new_2 = subtract(2, whole, decayed_2, clipped_2)
-        clipped_3 = clip_on_gpsimd(LAST, whole, 1)
+        raised_2 = clip_below(2, whole, 3, after_fetch("raised_2", whole, HALF))
+        clipped_2 = clip_above(raised_2, values("clipped", 2, whole, CLIPPED_2_AT))
+        decayed_2 = after_fetch("decayed_2", whole, 3 * HALF)
+        new_2 = values("new", 2, whole, None)
+        for piece in (first_half, second_half):
+            fetch_into(decayed_2[:, piece], piece, rows[2], -LIMIT)
+            nc.gpsimd.tensor_tensor(new_2[:, piece], decayed_2[:, piece], clipped_2[:, piece], ALU.add)
+        raised_3 = clip_below(LAST, whole, 3, values("raised", LAST, whole, RAISED_3_AT))
+        clipped_3 = clip_above(raised_3, values("clipped", LAST, whole, None))
+        decayed_3 = fetch(LAST, whole, rows[LAST], -LIMIT)
 
         grouped = [
-            reused.tile([P, CHUNK, PACK], BF16, name=f"grouped{c}", offset=CHUNK_AT[c], align_bytes=64)
+            reused.tile([P, CHUNK, PACK], BF16, name=f"grouped{c}", offset=c * CHUNK_BYTES, align_bytes=64)
             for c in range(CHUNKS)
         ]
 
@@ -230,15 +248,16 @@ def tile_picked_clipsgd_none_po_kernel(
 
         for c in range(VECTOR_CHUNKS):
             round_on_gpsimd(0, c)
-        decayed_3 = fetch(LAST, whole)
-        new_3 = subtract(LAST, whole, decayed_3, clipped_3, at=NEW_3_AT)
+        new_3 = values("new", LAST, whole, None)
+        nc.gpsimd.tensor_tensor(new_3[:], decayed_3[:], clipped_3[:], ALU.add)
         for c in range(VECTOR_CHUNKS, CHUNKS):
             round_on_scalar(0, c)
 
         def round_middle_turn(turn):
-            for c in range(CHUNKS - 1):
+            for c in range(VECTOR_CHUNKS):
                 round_on_scalar(turn, c)
-            round_on_gpsimd(turn, CHUNKS - 1)
+            for c in range(VECTOR_CHUNKS, CHUNKS):
+                round_on_gpsimd(turn, c)
 
         round_middle_turn(1)
         scatter(2, whole, new_2)

@@ -31,8 +31,8 @@ ROUNDED_AT = TABLE_AT + 4 * T
 SLOT = (2, 0, 1, 3)
 LAST = PACK - 1
 CHUNK = 256
-CHUNKS = U // CHUNK
-VECTOR_CHUNKS = 2
+GPSIMD_FROM = 608
+GROUPED_BYTES = PACK * U
 CUTS = (0, 256, 384, 512, 768, 1024)
 STORE_AT = (384, 768, 1024)
 
@@ -227,37 +227,33 @@ def tile_picked_clipsgd_none_po_kernel(
         decayed_3 = fetch(LAST, whole, rows[LAST], -LIMIT)
 
         grouped = [
-            reused.tile([P, CHUNK, PACK], BF16, name=f"grouped{c}", offset=c * CHUNK_BYTES, align_bytes=64)
-            for c in range(CHUNKS)
+            reused.tile([P, U // 2, PACK], BF16, name=f"grouped{h}", offset=h * GROUPED_BYTES, align_bytes=64)
+            for h in range(2)
         ]
 
-        def rounding(turn, c):
-            return grouped[c][:, :, SLOT[turn]], rows[turn][:, c * CHUNK : (c + 1) * CHUNK]
+        def words(first, stop):
+            h = first // (U // 2)
+            return grouped[h][:, first - h * U // 2 : stop - h * U // 2, :]
 
-        def round_on_scalar(turn, c):
-            out, in_ = rounding(turn, c)
-            nc.scalar.copy(out=out, in_=in_)
+        def round_on_scalar(turn, first, stop):
+            nc.scalar.copy(out=words(first, stop)[:, :, SLOT[turn]], in_=rows[turn][:, first:stop])
 
-        def round_on_vector(turn, c):
-            out, in_ = rounding(turn, c)
-            nc.vector.tensor_copy(out=out, in_=in_)
+        def round_on_vector(turn, first, stop):
+            nc.vector.tensor_copy(out=words(first, stop)[:, :, SLOT[turn]], in_=rows[turn][:, first:stop])
 
-        def round_on_gpsimd(turn, c):
-            out, in_ = rounding(turn, c)
-            nc.gpsimd.tensor_scalar(out, in_, 1.0, 1.0, ALU.mult, ALU.mult)
+        def round_on_gpsimd(turn, first, stop):
+            out = words(first, stop)[:, :, SLOT[turn]]
+            nc.gpsimd.tensor_scalar(out, rows[turn][:, first:stop], 1.0, 1.0, ALU.mult, ALU.mult)
 
-        for c in range(VECTOR_CHUNKS):
-            round_on_gpsimd(0, c)
+        round_on_gpsimd(0, 0, U // 2)
         new_3 = values("new", LAST, whole, None)
         nc.gpsimd.tensor_tensor(new_3[:], decayed_3[:], clipped_3[:], ALU.add)
-        for c in range(VECTOR_CHUNKS, CHUNKS):
-            round_on_scalar(0, c)
+        round_on_scalar(0, U // 2, U)
 
         def round_middle_turn(turn):
-            for c in range(VECTOR_CHUNKS):
-                round_on_scalar(turn, c)
-            for c in range(VECTOR_CHUNKS, CHUNKS):
-                round_on_gpsimd(turn, c)
+            round_on_scalar(turn, 0, U // 2)
+            round_on_scalar(turn, U // 2, GPSIMD_FROM)
+            round_on_gpsimd(turn, GPSIMD_FROM, U)
 
         round_middle_turn(1)
         scatter(2, whole, new_2)
@@ -265,21 +261,20 @@ def tile_picked_clipsgd_none_po_kernel(
         round_middle_turn(2)
         scatter(LAST, whole, new_3)
         store(LAST)
-        for c in range(VECTOR_CHUNKS):
-            round_on_vector(LAST, c)
-        for c in range(VECTOR_CHUNKS, CHUNKS):
-            round_on_scalar(LAST, c)
+        for first in range(0, U // 2, CHUNK):
+            round_on_vector(LAST, first, first + CHUNK)
+        for first in range(U // 2, U, CHUNK):
+            round_on_scalar(LAST, first, first + CHUNK)
 
         out_codes = keep.tile([P, U], U32, name="out_codes", align_bytes=64)
         out_scale = keep.tile([P, U], U8, name="out_scale", align_bytes=64)
         out_words = out_1[0].rearrange("p c r -> p (c r)").bitcast(I32)
         stored = 0
         for first, stop in zip(CUTS, CUTS[1:]):
-            c = first // CHUNK
             nc.vector.quantize_mx(
                 out=out_codes[:, first:stop].bitcast(FP8X4),
                 scales=out_scale[:, first:stop],
-                in_=grouped[c][:, first - c * CHUNK : stop - c * CHUNK, :].rearrange("p c s -> p (c s)"),
+                in_=words(first, stop).rearrange("p c s -> p (c s)"),
             )
             if stop in STORE_AT:
                 nc.sync.dma_start(out=out_words[:, stored:stop], in_=out_codes[:, stored:stop].bitcast(I32))

@@ -25,8 +25,8 @@ QUADRANTS = 4
 LIST_ROWS = 16
 W_BYTES = 4 * PACK * N
 ROW_BYTES = 4 * U
-TABLE_AT = PASSES * W_BYTES
-ROUNDED_AT = TABLE_AT + 4 * T
+ROUNDED_AT = T + PASSES * W_BYTES
+ROWS_AT = (0, ROW_BYTES, T + W_BYTES, T + W_BYTES + ROW_BYTES)
 
 SLOT = (2, 0, 1, 3)
 LAST = PACK - 1
@@ -55,8 +55,8 @@ def tile_picked_clipsgd_none_po_kernel(
 
         offs_sb = keep.tile([P, S // LIST_ROWS], U16, name="offs_sb")
         ent_sb = keep.tile([P, S // LIST_ROWS], U16, name="ent_sb")
-        w_raw = [loads.tile([P, PACK, N], F32, name=f"w_raw{z}", offset=z * W_BYTES) for z in range(PASSES)]
-        x_scale_table = loads.tile([P, T], U8, name="x_scale_table", offset=TABLE_AT)
+        w_raw = [loads.tile([P, PACK, N], F32, name=f"w_raw{z}", offset=T + z * W_BYTES) for z in range(PASSES)]
+        x_scale_table = loads.tile([P, T], U8, name="x_scale_table", offset=0)
         x_first = keep.tile([P, T], U32, name="x_table0", align_bytes=64)
         x_picked_scale = keep.tile([P, S], U8, name="x_picked_scale", align_bytes=64)
         x_scale = keep.tile([P, PASSES, S], U8, name="x_scale", align_bytes=64)
@@ -74,16 +74,17 @@ def tile_picked_clipsgd_none_po_kernel(
         nc.vector.memset(x_scale[:].rearrange("p z c -> p (z c)").bitcast(I32), 0)
 
         w_passes = w1.rearrange("(z p j) c -> z p j c", z=PASSES, j=PACK)
-        nc.sync.dma_start(out=w_raw[0][:, : PACK // 2, :], in_=w_passes[0][:, : PACK // 2, :])
+        nc.sync.dma_start(out=w_raw[0][:], in_=w_passes[0])
         nc.sync.dma_start(
             out=x_scale_table[0:P:4].bitcast(I32),
             in_=x_scales.rearrange("z q c -> q z c").bitcast(I32),
         )
         nc.sync.dma_start(offs_sb[:], offs)
-        nc.sync.dma_start(out=w_raw[0][:, PACK // 2 :, :], in_=w_passes[0][:, PACK // 2 :, :])
         nc.sync.dma_start(out=w_raw[1][:], in_=w_passes[1])
         load_x(x_first, 0)
         nc.sync.dma_start(ent_sb[:], ent)
+        x_last = keep.tile([P, T], U32, name="x_table1", align_bytes=64)
+        load_x(x_last, 1)
 
         nc.vector.tensor_copy(x_picked_scale[:], x_scale_table[:].indirect(offs_sb[:]))
         first_half, second_half, whole = slice(0, S // 2), slice(S // 2, S), slice(0, S)
@@ -95,9 +96,7 @@ def tile_picked_clipsgd_none_po_kernel(
             )
 
         for q in range(QUADRANTS):
-            move_scales(q, whole if q < QUADRANTS - 1 else first_half)
-        x_last = loads.tile([P, T], U32, name="x_table1", offset=TABLE_AT)
-        load_x(x_last, 1)
+            move_scales(q, first_half)
         x_table = [x_first, x_last]
 
         w_codes, w_scale = [], []
@@ -125,10 +124,11 @@ def tile_picked_clipsgd_none_po_kernel(
         out_rows = out_0.rearrange("(p s) c -> s p c", s=PACK)
         rows = []
         for turn in range(PACK):
-            rows.append(loads.tile([P, U], F32, name=f"rows{turn}", offset=turn * ROW_BYTES))
+            rows.append(loads.tile([P, U], F32, name=f"rows{turn}", offset=ROWS_AT[turn]))
             nc.sync.dma_start(out=rows[turn][:], in_=par_rows[SLOT[turn]])
             if turn == 1:
-                move_scales(QUADRANTS - 1, second_half)
+                for q in range(QUADRANTS):
+                    move_scales(q, second_half)
                 rows_again = loads.tile([P, U], F32, name="rows_again", offset=ROUNDED_AT)
                 nc.sync.dma_start(out=rows_again[:], in_=par_rows[SLOT[0]])
 

@@ -96,7 +96,7 @@ def tile_picked_clipsgd_none_po_kernel(
             )
 
         for q in range(QUADRANTS):
-            move_scales(q, first_half)
+            move_scales(q, whole if q < QUADRANTS - 1 else first_half)
         x_table = [x_first, x_last]
 
         w_codes, w_scale = [], []
@@ -127,8 +127,7 @@ def tile_picked_clipsgd_none_po_kernel(
             rows.append(loads.tile([P, U], F32, name=f"rows{turn}", offset=ROWS_AT[turn]))
             nc.sync.dma_start(out=rows[turn][:], in_=par_rows[SLOT[turn]])
             if turn == 1:
-                for q in range(QUADRANTS):
-                    move_scales(q, second_half)
+                move_scales(QUADRANTS - 1, second_half)
                 rows_again = loads.tile([P, U], F32, name="rows_again", offset=ROUNDED_AT)
                 nc.sync.dma_start(out=rows_again[:], in_=par_rows[SLOT[0]])
 

@@ -25,8 +25,8 @@ QUADRANTS = 4
 LIST_ROWS = 16
 W_BYTES = 4 * PACK * N
 ROW_BYTES = 4 * U
-ROUNDED_AT = T + PASSES * W_BYTES
-ROWS_AT = (0, ROW_BYTES, T + W_BYTES, T + W_BYTES + ROW_BYTES)
+X_LAST_AT = PASSES * W_BYTES
+ROUNDED_AT = X_LAST_AT + 4 * T
 
 SLOT = (2, 0, 1, 3)
 LAST = PACK - 1
@@ -55,8 +55,8 @@ def tile_picked_clipsgd_none_po_kernel(
 
         offs_sb = keep.tile([P, S // LIST_ROWS], U16, name="offs_sb")
         ent_sb = keep.tile([P, S // LIST_ROWS], U16, name="ent_sb")
-        w_raw = [loads.tile([P, PACK, N], F32, name=f"w_raw{z}", offset=T + z * W_BYTES) for z in range(PASSES)]
-        x_scale_table = loads.tile([P, T], U8, name="x_scale_table", offset=0)
+        w_raw = [loads.tile([P, PACK, N], F32, name=f"w_raw{z}", offset=z * W_BYTES) for z in range(PASSES)]
+        x_scale_table = loads.tile([P, T], U8, name="x_scale_table", offset=ROUNDED_AT - T // 2)
         x_first = keep.tile([P, T], U32, name="x_table0", align_bytes=64)
         x_picked_scale = keep.tile([P, S], U8, name="x_picked_scale", align_bytes=64)
         x_scale = keep.tile([P, PASSES, S], U8, name="x_scale", align_bytes=64)
@@ -83,8 +83,6 @@ def tile_picked_clipsgd_none_po_kernel(
         nc.sync.dma_start(out=w_raw[1][:], in_=w_passes[1])
         load_x(x_first, 0)
         nc.sync.dma_start(ent_sb[:], ent)
-        x_last = keep.tile([P, T], U32, name="x_table1", align_bytes=64)
-        load_x(x_last, 1)
 
         nc.vector.tensor_copy(x_picked_scale[:], x_scale_table[:].indirect(offs_sb[:]))
         first_half, second_half, whole = slice(0, S // 2), slice(S // 2, S), slice(0, S)
@@ -97,6 +95,8 @@ def tile_picked_clipsgd_none_po_kernel(
 
         for q in range(QUADRANTS):
             move_scales(q, whole if q < QUADRANTS - 1 else first_half)
+        x_last = loads.tile([P, T], U32, name="x_table1", offset=X_LAST_AT)
+        load_x(x_last, 1)
         x_table = [x_first, x_last]
 
         w_codes, w_scale = [], []
@@ -124,7 +124,7 @@ def tile_picked_clipsgd_none_po_kernel(
         out_rows = out_0.rearrange("(p s) c -> s p c", s=PACK)
         rows = []
         for turn in range(PACK):
-            rows.append(loads.tile([P, U], F32, name=f"rows{turn}", offset=ROWS_AT[turn]))
+            rows.append(loads.tile([P, U], F32, name=f"rows{turn}", offset=turn * ROW_BYTES))
             nc.sync.dma_start(out=rows[turn][:], in_=par_rows[SLOT[turn]])
             if turn == 1:
                 move_scales(QUADRANTS - 1, second_half)

@@ -131,9 +131,10 @@ def tile_picked_clipsgd_none_po_kernel(
                 rows_again = loads.tile([P, U], F32, name="rows_again", offset=ROUNDED_AT)
                 nc.sync.dma_start(out=rows_again[:], in_=par_rows[SLOT[0]])
 
+        quarters = (slice(0, S // 4), slice(S // 4, S // 2))
         x_codes = [keep.tile([P, S], U32, name=f"x_codes{z}", align_bytes=64) for z in range(PASSES)]
         for z in range(PASSES):
-            for piece in (first_half, second_half):
+            for piece in (first_half, second_half) if z == 0 else (*quarters, second_half):
                 nc.vector.tensor_copy(x_codes[z][:, piece], x_table[z][:].indirect(entries(offs_sb, piece)))
 
         def values(kind, turn, piece, at):
@@ -145,15 +146,20 @@ def tile_picked_clipsgd_none_po_kernel(
         def product(turn, piece, bank):
             y = psum.tile([P, piece.stop - piece.start], F32, name=f"y{turn}_{piece.start}", tag=f"bank{bank}")
             cols = slice(P * SLOT[turn], P * (SLOT[turn] + 1))
-            for z in range(PASSES):
+            if piece == first_half:
+                steps = [(first_half, 0), (quarters[0], 1), (quarters[1], 1)]
+            else:
+                halves = (first_half, second_half) if piece == whole else (piece,)
+                steps = [(half, z) for half in halves for z in range(PASSES)]
+            for step, (half, z) in enumerate(steps):
                 nc.tensor.matmul_mx(
-                    out=y[:],
+                    out=y[:, half.start - piece.start : half.stop - piece.start],
                     lhsT=w_codes[z][:, cols].bitcast(FP8X4),
                     lhsT_scale=w_scale[z][:, cols],
-                    rhs=x_codes[z][:, piece].bitcast(FP8X4),
-                    rhs_scale=x_scale[:, z, piece],
-                    start=(z == 0),
-                    stop=(z == PASSES - 1),
+                    rhs=x_codes[z][:, half].bitcast(FP8X4),
+                    rhs_scale=x_scale[:, z, half],
+                    start=(step == 0),
+                    stop=(step == len(steps) - 1),
                 )
             return y
 
@@ -221,13 +227,13 @@ def tile_picked_clipsgd_none_po_kernel(
         for piece in (first_half, second_half):
             fetch_into(decayed_2[:, piece], piece, rows[2], -LIMIT)
             nc.gpsimd.tensor_tensor(new_2[:, piece], decayed_2[:, piece], clipped_2[:, piece], ALU.add)
-        raised_3 = clip_below(LAST, whole, 3, values("raised", LAST, whole, RAISED_3_AT))
+        raised_3 = clip_below(LAST, whole, 5, after_fetch("raised_3", whole, HALF))
         clipped_3 = clip_above(raised_3, values("clipped", LAST, whole, None))
         decayed_3 = fetch(LAST, whole, rows[LAST], -LIMIT)
 
         grouped = [
-            reused.tile([P, U // 2, PACK], BF16, name=f"grouped{h}", offset=h * GROUPED_BYTES, align_bytes=64)
-            for h in range(2)
+            reused.tile([P, U // 2, PACK], BF16, name="grouped0", offset=0, align_bytes=64),
+            loads.tile([P, U // 2, PACK], BF16, name="grouped1", offset=ROUNDED_AT, align_bytes=64),
         ]
 
         def words(first, stop):

@@ -27,20 +27,15 @@ W_BYTES = 4 * PACK * N
 ROW_BYTES = 4 * U
 X_LAST_AT = PASSES * W_BYTES
 ROUNDED_AT = X_LAST_AT + 4 * T
+LIST_BYTES = 4 * S
+DECAYED_0B_AT, DECAYED_1_AT, DECAYED_2A_AT, DECAYED_3_AT, PLANES_AT = range(0, 5 * LIST_BYTES, LIST_BYTES)
 
-SLOT = (2, 0, 1, 3)
-LAST = PACK - 1
-CHUNK = 256
-GPSIMD_FROM = 608
-GROUPED_BYTES = PACK * U
-CUTS = (0, 256, 384, 512, 768, 1024)
-STORE_AT = (384, 768, 1024)
-
-HALF = 4 * S // 2
-CHUNK_BYTES = 2 * PACK * CHUNK
-CLIPPED_2_AT = CHUNK_BYTES - HALF
-RAISED_3_AT = 3 * CHUNK_BYTES - 3 * HALF // 2
-HANDED_ON_AT = 4 * CHUNK_BYTES
+SCALAR_FROM = 576
+VECTOR_WEAVES = (0, 256, 576)
+SCALAR_WEAVES = (576, 768, 1024)
+CUTS = (0, 256, 512, 768, 1024)
+STORE_AT = (512, 768, 1024)
+NEAR = 4
 
 
 def tile_picked_clipsgd_none_po_kernel(
@@ -86,15 +81,13 @@ def tile_picked_clipsgd_none_po_kernel(
 
         nc.vector.tensor_copy(x_picked_scale[:], x_scale_table[:].indirect(offs_sb[:]))
         first_half, second_half, whole = slice(0, S // 2), slice(S // 2, S), slice(0, S)
-
-        def move_scales(q, piece):
-            nc.sync.dma_start(
-                out=x_scale[32 * q : 32 * q + 4, :, piece].bitcast(I32),
-                in_=x_picked_scale[32 * q : 32 * q + 32 : 4, piece].bitcast(I32),
-            )
+        halves = (first_half, second_half)
 
         for q in range(QUADRANTS):
-            move_scales(q, whole if q < QUADRANTS - 1 else first_half)
+            nc.sync.dma_start(
+                out=x_scale[32 * q : 32 * q + 4].bitcast(I32),
+                in_=x_picked_scale[32 * q : 32 * q + 32 : 4].bitcast(I32),
+            )
         x_last = loads.tile([P, T], U32, name="x_table1", offset=X_LAST_AT)
         load_x(x_last, 1)
         x_table = [x_first, x_last]
@@ -107,9 +100,9 @@ def tile_picked_clipsgd_none_po_kernel(
             dealt = w_bf[:].rearrange("p s m j -> p m j s")
             source = w_raw[z][:].rearrange("p j (m s) -> p m j s", s=PACK)
             if z == 1:
-                nc.scalar.activation(out=dealt, in_=source, func=ACT.Copy, scale=-1.0)
+                nc.scalar.activation(out=dealt, in_=source, func=ACT.Copy)
             else:
-                nc.vector.tensor_scalar(dealt, source, -1.0, None, ALU.mult)
+                nc.vector.tensor_copy(dealt, source)
             codes = keep.tile([P, N], U32, name=f"w_codes{z}", align_bytes=64)
             scale = keep.tile([P, N], U8, name=f"w_scale{z}", align_bytes=64)
             nc.vector.quantize_mx(
@@ -123,153 +116,121 @@ def tile_picked_clipsgd_none_po_kernel(
         par_rows = par.rearrange("(p s) c -> s p c", s=PACK)
         out_rows = out_0.rearrange("(p s) c -> s p c", s=PACK)
         rows = []
-        for turn in range(PACK):
-            rows.append(loads.tile([P, U], F32, name=f"rows{turn}", offset=turn * ROW_BYTES))
-            nc.sync.dma_start(out=rows[turn][:], in_=par_rows[SLOT[turn]])
-            if turn == 1:
-                move_scales(QUADRANTS - 1, second_half)
-                rows_again = loads.tile([P, U], F32, name="rows_again", offset=ROUNDED_AT)
-                nc.sync.dma_start(out=rows_again[:], in_=par_rows[SLOT[0]])
+        for s in range(PACK):
+            rows.append(loads.tile([P, U], F32, name=f"rows{s}", offset=s * ROW_BYTES))
+            nc.sync.dma_start(out=rows[s][:], in_=par_rows[s])
 
-        quarters = (slice(0, S // 4), slice(S // 4, S // 2))
         x_codes = [keep.tile([P, S], U32, name=f"x_codes{z}", align_bytes=64) for z in range(PASSES)]
         for z in range(PASSES):
-            for piece in (first_half, second_half) if z == 0 else (*quarters, second_half):
+            for piece in halves:
                 nc.vector.tensor_copy(x_codes[z][:, piece], x_table[z][:].indirect(entries(offs_sb, piece)))
 
-        def values(kind, turn, piece, at):
-            shape, name = [P, piece.stop - piece.start], f"{kind}{turn}_{piece.start}"
+        clipped = [keep.tile([P, 2, S], F32, name=f"clipped{pair}") for pair in range(PACK // 2)]
+        for pair in range(PACK // 2):
+            for piece in halves:
+                y = psum.tile([P, 2, S // 2], F32, name=f"y{pair}_{piece.start}")
+                steps = [(z, i) for z in range(PASSES) for i in range(2)]
+                for step, (z, i) in enumerate(steps):
+                    cols = slice(P * (2 * pair + i), P * (2 * pair + i + 1))
+                    nc.tensor.matmul_mx(
+                        out=y[:, i, :],
+                        lhsT=w_codes[z][:, cols].bitcast(FP8X4),
+                        lhsT_scale=w_scale[z][:, cols],
+                        rhs=x_codes[z][:, piece].bitcast(FP8X4),
+                        rhs_scale=x_scale[:, z, piece],
+                        start=(step == 0),
+                        stop=(step == len(steps) - 1),
+                    )
+                nc.vector.tensor_scalar(clipped[pair][:, :, piece], y[:], LIMIT, -LIMIT, ALU.min, ALU.max)
+
+        def window(s, piece):
+            return rows[s][:].indirect(entries(ent_sb, piece))
+
+        def values(name, piece, at=None):
+            shape = [P, piece.stop - piece.start]
             if at is None:
                 return keep.tile(shape, F32, name=name)
             return reused.tile(shape, F32, name=name, offset=at)
 
-        def product(turn, piece, bank):
-            y = psum.tile([P, piece.stop - piece.start], F32, name=f"y{turn}_{piece.start}", tag=f"bank{bank}")
-            cols = slice(P * SLOT[turn], P * (SLOT[turn] + 1))
-            if piece == first_half:
-                steps = [(first_half, 0), (quarters[0], 1), (quarters[1], 1)]
-            else:
-                halves = (first_half, second_half) if piece == whole else (piece,)
-                steps = [(half, z) for half in halves for z in range(PASSES)]
-            for step, (half, z) in enumerate(steps):
-                nc.tensor.matmul_mx(
-                    out=y[:, half.start - piece.start : half.stop - piece.start],
-                    lhsT=w_codes[z][:, cols].bitcast(FP8X4),
-                    lhsT_scale=w_scale[z][:, cols],
-                    rhs=x_codes[z][:, half].bitcast(FP8X4),
-                    rhs_scale=x_scale[:, z, half],
-                    start=(step == 0),
-                    stop=(step == len(steps) - 1),
-                )
-            return y
+        def fetch_on_scalar(s, piece, decayed):
+            nc.scalar.activation(out=decayed, in_=window(s, piece), func=ACT.Copy, scale=DECAY)
 
-        def clip_on_vector(turn, piece, bank):
-            y = product(turn, piece, bank)
-            clipped = values("clipped", turn, piece, None)
-            nc.vector.tensor_scalar(clipped[:], y[:], LIMIT, -LIMIT, ALU.min, ALU.max)
-            return clipped
+        def fetch_on_vector(s, piece, decayed):
+            nc.vector.tensor_scalar(decayed, window(s, piece), DECAY, 0.0, ALU.mult, ALU.add)
 
-        def after_fetch(name, piece, at):
-            return loads.tile([P, piece.stop - piece.start], F32, name=name, offset=ROUNDED_AT + at)
+        def subtract(s, piece, new, decayed):
+            nc.gpsimd.tensor_tensor(new, decayed, clipped[s // 2][:, s % 2, piece], ALU.subtract)
 
-        def clip_below(turn, piece, bank, raised):
-            y = product(turn, piece, bank)
-            nc.scalar.activation(out=raised[:], in_=y[:], func=ACT.Relu, scale=-1.0, bias=LIMIT)
-            return raised
+        def scatter_on_vector(s, piece, new):
+            nc.vector.tensor_copy(window(s, piece), new)
 
-        def clip_above(raised, clipped):
-            nc.scalar.activation(out=clipped[:], in_=raised[:], func=ACT.Relu, scale=-1.0, bias=2 * LIMIT)
-            return clipped
+        def scatter_on_scalar(s, piece, new):
+            nc.scalar.activation(out=window(s, piece), in_=new, func=ACT.Copy)
 
-        def fetch_into(out, piece, window, shift):
-            nc.scalar.activation(
-                out=out, in_=window[:].indirect(entries(ent_sb, piece)), func=ACT.Copy, scale=DECAY, bias=shift
-            )
+        def store(s):
+            nc.sync.dma_start(out=out_rows[s], in_=rows[s][:])
 
-        def fetch(turn, piece, window, shift):
-            decayed = values("decayed", turn, piece, None)
-            fetch_into(decayed[:], piece, window, shift)
-            return decayed
+        decayed_0a = values("decayed_0a", first_half)
+        decayed_0b = values("decayed_0b", second_half, DECAYED_0B_AT)
+        new_0a = values("new_0a", first_half)
+        fetch_on_scalar(0, first_half, decayed_0a[:])
+        fetch_on_scalar(0, second_half, decayed_0b[:])
+        subtract(0, first_half, new_0a[:], decayed_0a[:])
+        scatter_on_vector(0, first_half, new_0a[:])
 
-        def scatter(turn, piece, new):
-            nc.vector.tensor_copy(rows[turn][:].indirect(entries(ent_sb, piece)), new[:])
+        decayed_1 = values("decayed_1", whole, DECAYED_1_AT)
+        fetch_on_scalar(1, whole, decayed_1[:])
 
-        def scatter_sum(turn, piece, decayed, clipped):
-            nc.vector.tensor_tensor(rows[turn][:].indirect(entries(ent_sb, piece)), decayed[:], clipped[:], ALU.add)
-
-        def store(turn):
-            nc.sync.dma_start(out=out_rows[SLOT[turn]], in_=rows[turn][:])
-
-        clipped_0a = clip_on_vector(0, first_half, 0)
-        clipped_1a = clip_on_vector(1, first_half, 1)
-        decayed_0a = fetch(0, first_half, rows[0], 0.0)
-        scatter_sum(0, first_half, decayed_0a, clipped_0a)
-        decayed_1a = fetch(1, first_half, rows[1], 0.0)
-        decayed_1b = fetch(1, second_half, rows[1], -LIMIT)
-        scatter_sum(1, first_half, decayed_1a, clipped_1a)
-        raised_0b = clip_below(0, second_half, 2, values("raised", 0, second_half, HANDED_ON_AT))
-        decayed_0b = fetch(0, second_half, rows_again, -LIMIT)
-        y_1b = product(1, second_half, 4)
-        capped_1b = values("capped", 1, second_half, None)
-        nc.scalar.activation(out=capped_1b[:], in_=y_1b[:], func=ACT.Relu, bias=LIMIT)
-        clipped_0b = clip_above(raised_0b, after_fetch("clipped_0b", second_half, 0))
-        new_1b = values("new", 1, second_half, HANDED_ON_AT)
-        nc.vector.scalar_tensor_tensor(new_1b[:], capped_1b[:], 2 * LIMIT, decayed_1b[:], ALU.min, ALU.add)
-        scatter_sum(0, second_half, decayed_0b, clipped_0b)
-        store(0)
-        scatter(1, second_half, new_1b)
+        upper_at = PLANES_AT + 2 * PACK * SCALAR_FROM
+        decayed_2a = values("decayed_2a", first_half, DECAYED_2A_AT)
+        decayed_2b = values("decayed_2b", second_half, upper_at - LIST_BYTES // 4)
+        new_2a = values("new_2a", first_half)
+        fetch_on_scalar(2, first_half, decayed_2a[:])
+        fetch_on_scalar(2, second_half, decayed_2b[:])
+        subtract(2, first_half, new_2a[:], decayed_2a[:])
+        scatter_on_scalar(2, first_half, new_2a[:])
+        new_1 = values("new_1", whole, DECAYED_2A_AT)
+        subtract(1, whole, new_1[:], decayed_1[:])
+        scatter_on_scalar(1, whole, new_1[:])
         store(1)
 
-        raised_2 = clip_below(2, whole, 3, after_fetch("raised_2", whole, HALF))
-        clipped_2 = clip_above(raised_2, values("clipped", 2, whole, CLIPPED_2_AT))
-        decayed_2 = after_fetch("decayed_2", whole, 3 * HALF)
-        new_2 = values("new", 2, whole, None)
-        for piece in (first_half, second_half):
-            fetch_into(decayed_2[:, piece], piece, rows[2], -LIMIT)
-            nc.gpsimd.tensor_tensor(new_2[:, piece], decayed_2[:, piece], clipped_2[:, piece], ALU.add)
-        raised_3 = clip_below(LAST, whole, 5, after_fetch("raised_3", whole, HALF))
-        clipped_3 = clip_above(raised_3, values("clipped", LAST, whole, None))
-        decayed_3 = fetch(LAST, whole, rows[LAST], -LIMIT)
-
-        grouped = [
-            reused.tile([P, U // 2, PACK], BF16, name="grouped0", offset=0, align_bytes=64),
-            loads.tile([P, U // 2, PACK], BF16, name="grouped1", offset=ROUNDED_AT, align_bytes=64),
-        ]
-
-        def words(first, stop):
-            h = first // (U // 2)
-            return grouped[h][:, first - h * U // 2 : stop - h * U // 2, :]
-
-        def round_on_scalar(turn, first, stop):
-            nc.scalar.copy(out=words(first, stop)[:, :, SLOT[turn]], in_=rows[turn][:, first:stop])
-
-        def round_on_vector(turn, first, stop):
-            nc.vector.tensor_copy(out=words(first, stop)[:, :, SLOT[turn]], in_=rows[turn][:, first:stop])
-
-        def round_on_gpsimd(turn, first, stop):
-            out = words(first, stop)[:, :, SLOT[turn]]
-            nc.gpsimd.tensor_scalar(out, rows[turn][:, first:stop], 1.0, 1.0, ALU.mult, ALU.mult)
-
-        round_on_gpsimd(0, 0, U // 2)
-        new_3 = values("new", LAST, whole, None)
-        nc.gpsimd.tensor_tensor(new_3[:], decayed_3[:], clipped_3[:], ALU.add)
-        round_on_scalar(0, U // 2, U)
-
-        def round_middle_turn(turn):
-            round_on_scalar(turn, 0, U // 2)
-            round_on_scalar(turn, U // 2, GPSIMD_FROM)
-            round_on_gpsimd(turn, GPSIMD_FROM, U)
-
-        round_middle_turn(1)
-        scatter(2, whole, new_2)
+        decayed_3 = values("decayed_3", whole, DECAYED_3_AT)
+        fetch_on_vector(3, whole, decayed_3[:])
+        new_0b = values("new_0b", second_half, DECAYED_1_AT)
+        subtract(0, second_half, new_0b[:], decayed_0b[:])
+        scatter_on_vector(0, second_half, new_0b[:])
+        store(0)
+        new_3 = values("new_3", whole, DECAYED_0B_AT)
+        subtract(3, whole, new_3[:], decayed_3[:])
+        scatter_on_vector(3, whole, new_3[:])
+        new_2b = values("new_2b", second_half, DECAYED_3_AT)
+        subtract(2, second_half, new_2b[:], decayed_2b[:])
+        scatter_on_scalar(2, second_half, new_2b[:])
         store(2)
-        round_middle_turn(2)
-        scatter(LAST, whole, new_3)
-        store(LAST)
-        for first in range(0, U // 2, CHUNK):
-            round_on_vector(LAST, first, first + CHUNK)
-        for first in range(U // 2, U, CHUNK):
-            round_on_scalar(LAST, first, first + CHUNK)
+        store(3)
+
+        lower = reused.tile([P, PACK, SCALAR_FROM], BF16, name="lower", offset=PLANES_AT)
+        upper = reused.tile([P, PACK, U - SCALAR_FROM], BF16, name="upper", offset=upper_at)
+        for s in (0, 1):
+            nc.gpsimd.tensor_scalar(lower[:, s, :], rows[s][:, :SCALAR_FROM], 1.0, 1.0, ALU.mult, ALU.mult)
+            nc.gpsimd.tensor_scalar(upper[:, s, :], rows[s][:, SCALAR_FROM:], 1.0, 1.0, ALU.mult, ALU.mult)
+        for s in (3, 2):
+            nc.vector.tensor_copy(lower[:, s, :], rows[s][:, :SCALAR_FROM])
+        for s in (2, 3):
+            nc.scalar.copy(upper[:, s, :], rows[s][:, SCALAR_FROM:])
+
+        grouped = keep.tile([P, U, PACK], BF16, name="grouped", align_bytes=64)
+
+        def weave(copy, planes, origin, first, stop):
+            copy(
+                out=grouped[:, first:stop, :].rearrange("p (c i) s -> p c s i", i=NEAR),
+                in_=planes[:, :, first - origin : stop - origin].rearrange("p s (c i) -> p c s i", i=NEAR),
+            )
+
+        for first, stop in zip(VECTOR_WEAVES, VECTOR_WEAVES[1:]):
+            weave(nc.vector.tensor_copy, lower, 0, first, stop)
+        for first, stop in zip(SCALAR_WEAVES, SCALAR_WEAVES[1:]):
+            weave(nc.scalar.copy, upper, SCALAR_FROM, first, stop)
 
         out_codes = keep.tile([P, U], U32, name="out_codes", align_bytes=64)
         out_scale = keep.tile([P, U], U8, name="out_scale", align_bytes=64)
@@ -279,7 +240,7 @@ def tile_picked_clipsgd_none_po_kernel(
             nc.vector.quantize_mx(
                 out=out_codes[:, first:stop].bitcast(FP8X4),
                 scales=out_scale[:, first:stop],
-                in_=words(first, stop).rearrange("p c s -> p (c s)"),
+                in_=grouped[:, first:stop, :].rearrange("p c s -> p (c s)"),
             )
             if stop in STORE_AT:
                 nc.sync.dma_start(out=out_words[:, stored:stop], in_=out_codes[:, stored:stop].bitcast(I32))

@@ -27,14 +27,14 @@ W_BYTES = 4 * PACK * N
 ROW_BYTES = 4 * U
 X_LAST_AT = PASSES * W_BYTES
 ROUNDED_AT = X_LAST_AT + 4 * T
-LIST_BYTES = 4 * S
-DECAYED_0B_AT, DECAYED_1_AT, DECAYED_2A_AT, DECAYED_3_AT, PLANES_AT = range(0, 5 * LIST_BYTES, LIST_BYTES)
+HALF_BYTES = 4 * S // 2
+PLANES_AT = HALF_BYTES
 
 SCALAR_FROM = 576
 VECTOR_WEAVES = (0, 256, 576)
-SCALAR_WEAVES = (576, 768, 1024)
-CUTS = (0, 256, 512, 768, 1024)
-STORE_AT = (512, 768, 1024)
+SCALAR_WEAVES = (576, 768, 896, 1024)
+CUTS = (0, 256, 640, 896, 1024)
+STORE_AT = (640, 896, 1024)
 NEAR = 4
 
 
@@ -115,10 +115,11 @@ def tile_picked_clipsgd_none_po_kernel(
 
         par_rows = par.rearrange("(p s) c -> s p c", s=PACK)
         out_rows = out_0.rearrange("(p s) c -> s p c", s=PACK)
-        rows = []
-        for s in range(PACK):
-            rows.append(loads.tile([P, U], F32, name=f"rows{s}", offset=s * ROW_BYTES))
-            nc.sync.dma_start(out=rows[s][:], in_=par_rows[s])
+        early = {s: loads.tile([P, U], F32, name=f"early{s}", offset=s * ROW_BYTES) for s in (1, 2)}
+        rows_at = (0, ROUNDED_AT, ROUNDED_AT + ROW_BYTES, 3 * ROW_BYTES)
+        rows = [loads.tile([P, U], F32, name=f"rows{s}", offset=rows_at[s]) for s in range(PACK)]
+        for tile, s in ((rows[0], 0), (early[1], 1), (early[2], 2), (rows[1], 1), (rows[3], 3), (rows[2], 2)):
+            nc.sync.dma_start(out=tile[:], in_=par_rows[s])
 
         x_codes = [keep.tile([P, S], U32, name=f"x_codes{z}", align_bytes=64) for z in range(PASSES)]
         for z in range(PASSES):
@@ -143,8 +144,8 @@ def tile_picked_clipsgd_none_po_kernel(
                     )
                 nc.vector.tensor_scalar(clipped[pair][:, :, piece], y[:], LIMIT, -LIMIT, ALU.min, ALU.max)
 
-        def window(s, piece):
-            return rows[s][:].indirect(entries(ent_sb, piece))
+        def window(tile, piece):
+            return tile[:].indirect(entries(ent_sb, piece))
 
         def values(name, piece, at=None):
             shape = [P, piece.stop - piece.start]
@@ -152,71 +153,71 @@ def tile_picked_clipsgd_none_po_kernel(
                 return keep.tile(shape, F32, name=name)
             return reused.tile(shape, F32, name=name, offset=at)
 
-        def fetch_on_scalar(s, piece, decayed):
-            nc.scalar.activation(out=decayed, in_=window(s, piece), func=ACT.Copy, scale=DECAY)
+        def fetch_on_scalar(tile, piece, decayed):
+            nc.scalar.activation(out=decayed, in_=window(tile, piece), func=ACT.Copy, scale=DECAY)
 
-        def fetch_on_vector(s, piece, decayed):
-            nc.vector.tensor_scalar(decayed, window(s, piece), DECAY, 0.0, ALU.mult, ALU.add)
+        def fetch_on_vector(tile, piece, decayed):
+            nc.vector.tensor_scalar(decayed, window(tile, piece), DECAY, 0.0, ALU.mult, ALU.add)
 
         def subtract(s, piece, new, decayed):
             nc.gpsimd.tensor_tensor(new, decayed, clipped[s // 2][:, s % 2, piece], ALU.subtract)
 
         def scatter_on_vector(s, piece, new):
-            nc.vector.tensor_copy(window(s, piece), new)
+            nc.vector.tensor_copy(window(rows[s], piece), new)
 
         def scatter_on_scalar(s, piece, new):
-            nc.scalar.activation(out=window(s, piece), in_=new, func=ACT.Copy)
+            nc.scalar.activation(out=window(rows[s], piece), in_=new, func=ACT.Copy)
 
         def store(s):
             nc.sync.dma_start(out=out_rows[s], in_=rows[s][:])
 
-        decayed_0a = values("decayed_0a", first_half)
-        decayed_0b = values("decayed_0b", second_half, DECAYED_0B_AT)
+        upper_at = PLANES_AT + 2 * PACK * SCALAR_FROM
+        decayed_0 = values("decayed_0", whole)
         new_0a = values("new_0a", first_half)
-        fetch_on_scalar(0, first_half, decayed_0a[:])
-        fetch_on_scalar(0, second_half, decayed_0b[:])
-        subtract(0, first_half, new_0a[:], decayed_0a[:])
+        for piece in halves:
+            fetch_on_scalar(rows[0], piece, decayed_0[:, piece])
+        subtract(0, first_half, new_0a[:], decayed_0[:, first_half])
         scatter_on_vector(0, first_half, new_0a[:])
 
-        decayed_1 = values("decayed_1", whole, DECAYED_1_AT)
-        fetch_on_scalar(1, whole, decayed_1[:])
-
-        upper_at = PLANES_AT + 2 * PACK * SCALAR_FROM
-        decayed_2a = values("decayed_2a", first_half, DECAYED_2A_AT)
-        decayed_2b = values("decayed_2b", second_half, upper_at - LIST_BYTES // 4)
-        new_2a = values("new_2a", first_half)
-        fetch_on_scalar(2, first_half, decayed_2a[:])
-        fetch_on_scalar(2, second_half, decayed_2b[:])
-        subtract(2, first_half, new_2a[:], decayed_2a[:])
-        scatter_on_scalar(2, first_half, new_2a[:])
-        new_1 = values("new_1", whole, DECAYED_2A_AT)
-        subtract(1, whole, new_1[:], decayed_1[:])
+        decayed_1 = values("decayed_1", whole)
+        new_1 = values("new_1", whole)
+        for piece in halves:
+            fetch_on_scalar(early[1], piece, decayed_1[:, piece])
+            subtract(1, piece, new_1[:, piece], decayed_1[:, piece])
+        decayed_2 = values("decayed_2", whole)
+        new_2 = values("new_2", whole)
+        fetch_on_scalar(early[2], whole, decayed_2[:])
+        subtract(2, whole, new_2[:], decayed_2[:])
         scatter_on_scalar(1, whole, new_1[:])
         store(1)
 
-        decayed_3 = values("decayed_3", whole, DECAYED_3_AT)
-        fetch_on_vector(3, whole, decayed_3[:])
-        new_0b = values("new_0b", second_half, DECAYED_1_AT)
-        subtract(0, second_half, new_0b[:], decayed_0b[:])
-        scatter_on_vector(0, second_half, new_0b[:])
-        store(0)
-        new_3 = values("new_3", whole, DECAYED_0B_AT)
-        subtract(3, whole, new_3[:], decayed_3[:])
-        scatter_on_vector(3, whole, new_3[:])
-        new_2b = values("new_2b", second_half, DECAYED_3_AT)
-        subtract(2, second_half, new_2b[:], decayed_2b[:])
-        scatter_on_scalar(2, second_half, new_2b[:])
+        decayed_3 = values("decayed_3", whole, upper_at - HALF_BYTES)
+        new_3 = values("new_3", whole)
+        for piece in halves:
+            fetch_on_vector(rows[3], piece, decayed_3[:, piece])
+            subtract(3, piece, new_3[:, piece], decayed_3[:, piece])
+        scatter_on_vector(2, whole, new_2[:])
         store(2)
-        store(3)
+        scatter_on_scalar(3, whole, new_3[:])
 
-        lower = reused.tile([P, PACK, SCALAR_FROM], BF16, name="lower", offset=PLANES_AT)
-        upper = reused.tile([P, PACK, U - SCALAR_FROM], BF16, name="upper", offset=upper_at)
-        for s in (0, 1):
+        lower = reused.tile([P, PACK, SCALAR_FROM], BF16, name="lower", offset=upper_at - HALF_BYTES // 2 - 2 * PACK * SCALAR_FROM)
+        upper = reused.tile([P, PACK, U - SCALAR_FROM], BF16, name="upper", offset=upper_at + HALF_BYTES // 2)
+
+        def round_on_gpsimd(s):
             nc.gpsimd.tensor_scalar(lower[:, s, :], rows[s][:, :SCALAR_FROM], 1.0, 1.0, ALU.mult, ALU.mult)
             nc.gpsimd.tensor_scalar(upper[:, s, :], rows[s][:, SCALAR_FROM:], 1.0, 1.0, ALU.mult, ALU.mult)
-        for s in (3, 2):
-            nc.vector.tensor_copy(lower[:, s, :], rows[s][:, :SCALAR_FROM])
-        for s in (2, 3):
+
+        new_0b = values("new_0b", second_half, upper_at - HALF_BYTES // 2)
+        subtract(0, second_half, new_0b[:], decayed_0[:, second_half])
+        scatter_on_vector(0, second_half, new_0b[:])
+        round_on_gpsimd(1)
+        round_on_gpsimd(2)
+        store(3)
+        store(0)
+        nc.vector.tensor_copy(lower[:, 3, :], rows[3][:, :SCALAR_FROM])
+        for first, stop in zip(VECTOR_WEAVES, VECTOR_WEAVES[1:]):
+            nc.vector.tensor_copy(lower[:, 0, first:stop], rows[0][:, first:stop])
+        for s in (3, 0):
             nc.scalar.copy(upper[:, s, :], rows[s][:, SCALAR_FROM:])
 
         grouped = keep.tile([P, U, PACK], BF16, name="grouped", align_bytes=64)

@@ -28,13 +28,11 @@ ROW_BYTES = 4 * U
 X_LAST_AT = PASSES * W_BYTES
 ROUNDED_AT = X_LAST_AT + 4 * T
 HALF_BYTES = 4 * S // 2
-PLANES_AT = HALF_BYTES
 
-SCALAR_FROM = 576
-VECTOR_WEAVES = (0, 256, 576)
-SCALAR_WEAVES = (576, 768, 896, 1024)
-CUTS = (0, 256, 640, 896, 1024)
-STORE_AT = (640, 896, 1024)
+VECTOR_WEAVES = (0, 256, 512, 672)
+SCALAR_WEAVES = (672, 896, 1024)
+CUTS = (0, 512, 896, 1024)
+STORE_AT = (512, 896, 1024)
 NEAR = 4
 
 
@@ -171,7 +169,6 @@ def tile_picked_clipsgd_none_po_kernel(
         def store(s):
             nc.sync.dma_start(out=out_rows[s], in_=rows[s][:])
 
-        upper_at = PLANES_AT + 2 * PACK * SCALAR_FROM
         decayed_0 = values("decayed_0", whole)
         new_0a = values("new_0a", first_half)
         for piece in halves:
@@ -191,7 +188,7 @@ def tile_picked_clipsgd_none_po_kernel(
         scatter_on_scalar(1, whole, new_1[:])
         store(1)
 
-        decayed_3 = values("decayed_3", whole, upper_at - HALF_BYTES)
+        decayed_3 = values("decayed_3", whole, 0)
         new_3 = values("new_3", whole)
         for piece in halves:
             fetch_on_vector(rows[3], piece, decayed_3[:, piece])
@@ -200,38 +197,34 @@ def tile_picked_clipsgd_none_po_kernel(
         store(2)
         scatter_on_scalar(3, whole, new_3[:])
 
-        lower = reused.tile([P, PACK, SCALAR_FROM], BF16, name="lower", offset=upper_at - HALF_BYTES // 2 - 2 * PACK * SCALAR_FROM)
-        upper = reused.tile([P, PACK, U - SCALAR_FROM], BF16, name="upper", offset=upper_at + HALF_BYTES // 2)
-
-        def round_on_gpsimd(s):
-            nc.gpsimd.tensor_scalar(lower[:, s, :], rows[s][:, :SCALAR_FROM], 1.0, 1.0, ALU.mult, ALU.mult)
-            nc.gpsimd.tensor_scalar(upper[:, s, :], rows[s][:, SCALAR_FROM:], 1.0, 1.0, ALU.mult, ALU.mult)
-
-        new_0b = values("new_0b", second_half, upper_at - HALF_BYTES // 2)
+        new_0b = values("new_0b", second_half, 0)
         subtract(0, second_half, new_0b[:], decayed_0[:, second_half])
         scatter_on_vector(0, second_half, new_0b[:])
-        round_on_gpsimd(1)
-        round_on_gpsimd(2)
+        planes = reused.tile([P, 2, PACK, U // 2], BF16, name="planes", offset=HALF_BYTES)
+        for s in (1, 2):
+            halved = rows[s][:].rearrange("p (h c) -> p h c", h=2)
+            nc.gpsimd.tensor_scalar(planes[:, :, s, :], halved, 1.0, 1.0, ALU.mult, ALU.mult)
         store(3)
         store(0)
-        nc.vector.tensor_copy(lower[:, 3, :], rows[3][:, :SCALAR_FROM])
-        for first, stop in zip(VECTOR_WEAVES, VECTOR_WEAVES[1:]):
-            nc.vector.tensor_copy(lower[:, 0, first:stop], rows[0][:, first:stop])
+        nc.vector.tensor_copy(planes[:, 0, 3, :], rows[3][:, : U // 2])
+        for first, stop in zip(VECTOR_WEAVES, VECTOR_WEAVES[1:-1]):
+            nc.vector.tensor_copy(planes[:, 0, 0, first:stop], rows[0][:, first:stop])
         for s in (3, 0):
-            nc.scalar.copy(upper[:, s, :], rows[s][:, SCALAR_FROM:])
+            nc.scalar.copy(planes[:, 1, s, :], rows[s][:, U // 2 :])
 
         grouped = keep.tile([P, U, PACK], BF16, name="grouped", align_bytes=64)
 
-        def weave(copy, planes, origin, first, stop):
+        def weave(copy, first, stop):
+            h, origin = first // (U // 2), first // (U // 2) * (U // 2)
             copy(
                 out=grouped[:, first:stop, :].rearrange("p (c i) s -> p c s i", i=NEAR),
-                in_=planes[:, :, first - origin : stop - origin].rearrange("p s (c i) -> p c s i", i=NEAR),
+                in_=planes[:, h, :, first - origin : stop - origin].rearrange("p s (c i) -> p c s i", i=NEAR),
             )
 
         for first, stop in zip(VECTOR_WEAVES, VECTOR_WEAVES[1:]):
-            weave(nc.vector.tensor_copy, lower, 0, first, stop)
+            weave(nc.vector.tensor_copy, first, stop)
         for first, stop in zip(SCALAR_WEAVES, SCALAR_WEAVES[1:]):
-            weave(nc.scalar.copy, upper, SCALAR_FROM, first, stop)
+            weave(nc.scalar.copy, first, stop)
 
         out_codes = keep.tile([P, U], U32, name="out_codes", align_bytes=64)
         out_scale = keep.tile([P, U], U8, name="out_scale", align_bytes=64)

@@ -33,7 +33,7 @@ VECTOR_WEAVES = (0, 256, 512, 672)
 SCALAR_WEAVES = (672, 896, 1024)
 CUTS = (0, 512, 896, 1024)
 STORE_AT = (512, 896, 1024)
-NEAR = 4
+NEAR = 8
 
 
 def tile_picked_clipsgd_none_po_kernel(

@@ -29,10 +29,8 @@ X_LAST_AT = PASSES * W_BYTES
 ROUNDED_AT = X_LAST_AT + 4 * T
 HALF_BYTES = 4 * S // 2
 
-VECTOR_WEAVES = (0, 256, 512, 672)
-SCALAR_WEAVES = (672, 896, 1024)
-CUTS = (0, 512, 896, 1024)
-STORE_AT = (512, 896, 1024)
+CHUNK = 256
+SCALAR_LAST = 928
 NEAR = 8
 
 
@@ -207,8 +205,8 @@ def tile_picked_clipsgd_none_po_kernel(
         store(3)
         store(0)
         nc.vector.tensor_copy(planes[:, 0, 3, :], rows[3][:, : U // 2])
-        for first, stop in zip(VECTOR_WEAVES, VECTOR_WEAVES[1:-1]):
-            nc.vector.tensor_copy(planes[:, 0, 0, first:stop], rows[0][:, first:stop])
+        for first in (0, CHUNK):
+            nc.vector.tensor_copy(planes[:, 0, 0, first : first + CHUNK], rows[0][:, first : first + CHUNK])
         for s in (3, 0):
             nc.scalar.copy(planes[:, 1, s, :], rows[s][:, U // 2 :])
 
@@ -221,24 +219,31 @@ def tile_picked_clipsgd_none_po_kernel(
                 in_=planes[:, h, :, first - origin : stop - origin].rearrange("p s (c i) -> p c s i", i=NEAR),
             )
 
-        for first, stop in zip(VECTOR_WEAVES, VECTOR_WEAVES[1:]):
-            weave(nc.vector.tensor_copy, first, stop)
-        for first, stop in zip(SCALAR_WEAVES, SCALAR_WEAVES[1:]):
-            weave(nc.scalar.copy, first, stop)
-
         out_codes = keep.tile([P, U], U32, name="out_codes", align_bytes=64)
         out_scale = keep.tile([P, U], U8, name="out_scale", align_bytes=64)
         out_words = out_1[0].rearrange("p c r -> p (c r)").bitcast(I32)
-        stored = 0
-        for first, stop in zip(CUTS, CUTS[1:]):
+
+        def quantise(first, stop):
             nc.vector.quantize_mx(
                 out=out_codes[:, first:stop].bitcast(FP8X4),
                 scales=out_scale[:, first:stop],
                 in_=grouped[:, first:stop, :].rearrange("p c s -> p (c s)"),
             )
-            if stop in STORE_AT:
-                nc.sync.dma_start(out=out_words[:, stored:stop], in_=out_codes[:, stored:stop].bitcast(I32))
-                stored = stop
+
+        def store_codes(first, stop):
+            nc.sync.dma_start(out=out_words[:, first:stop], in_=out_codes[:, first:stop].bitcast(I32))
+
+        for first in (0, CHUNK):
+            weave(nc.vector.tensor_copy, first, first + CHUNK)
+        for first in (0, CHUNK):
+            quantise(first, first + CHUNK)
+        store_codes(0, 2 * CHUNK)
+        weave(nc.scalar.copy, 2 * CHUNK, 3 * CHUNK)
+        weave(nc.vector.tensor_copy, 3 * CHUNK, SCALAR_LAST)
+        weave(nc.scalar.copy, SCALAR_LAST, U)
+        for first in (2 * CHUNK, 3 * CHUNK):
+            quantise(first, first + CHUNK)
+            store_codes(first, first + CHUNK)
         for q in range(QUADRANTS):
             queue = nc.scalar if q % 2 else nc.sync
             queue.dma_start(

@@ -30,7 +30,7 @@ ROUNDED_AT = X_LAST_AT + 4 * T
 HALF_BYTES = 4 * S // 2
 
 CHUNK = 256
-SCALAR_LAST = 928
+SCALAR_LAST = 896
 NEAR = 8
 
 

from contextlib import ExitStack

import concourse.mybir as mybir

K, T, S, N, U = 1024, 2048, 512, 512, 1024
FLOPS = 2 * K * N * S

F32 = mybir.dt.float32
BF16 = mybir.dt.bfloat16
I32 = mybir.dt.int32
U32 = mybir.dt.uint32
U16 = mybir.dt.uint16
U8 = mybir.dt.uint8
FP8X4 = mybir.dt.float8_e4m3fn_x4
ALU = mybir.AluOpType
ACT = mybir.ActivationFunctionType

DECAY = 0.875
LIMIT = 0.75

P = 128
PACK = 4
PASSES = K // (P * PACK)
QUADRANTS = 4
LIST_ROWS = 16
W_BYTES = 4 * PACK * N
ROW_BYTES = 4 * U
X_LAST_AT = PASSES * W_BYTES
ROUNDED_AT = X_LAST_AT + 4 * T
HALF_BYTES = 4 * S // 2

CHUNK = 256
SCALAR_LAST = 896
NEAR = 8


def tile_picked_clipsgd_none_po_kernel(
    tc, x_words, x_scales, w1, par, offs, ent, out_0, out_1, out_2
):
    nc = tc.nc
    with ExitStack() as ctx:
        keep = ctx.enter_context(tc.tile_pool(name="keep", bufs=1))
        psum = ctx.enter_context(tc.psum_pool(name="psum", bufs=1))
        loads = ctx.enter_context(tc.tile_pool(name="loads", bufs=1))
        reused = ctx.enter_context(tc.tile_pool(name="reused", bufs=1))

        offs_sb = keep.tile([P, S // LIST_ROWS], U16, name="offs_sb")
        ent_sb = keep.tile([P, S // LIST_ROWS], U16, name="ent_sb")
        w_raw = [loads.tile([P, PACK, N], F32, name=f"w_raw{z}", offset=z * W_BYTES) for z in range(PASSES)]
        x_scale_table = loads.tile([P, T], U8, name="x_scale_table", offset=ROUNDED_AT - T // 2)
        x_first = keep.tile([P, T], U32, name="x_table0", align_bytes=64)
        x_picked_scale = keep.tile([P, S], U8, name="x_picked_scale", align_bytes=64)
        x_scale = keep.tile([P, PASSES, S], U8, name="x_scale", align_bytes=64)

        def entries(list_sb, piece):
            return list_sb[:, piece.start // LIST_ROWS : piece.stop // LIST_ROWS]

        def load_x(table, z):
            nc.sync.dma_start(
                out=table[:].bitcast(I32),
                in_=x_words[z].rearrange("p c r -> p (c r)").bitcast(I32),
            )

        nc.vector.memset(x_scale_table[:].bitcast(I32), 0)
        nc.vector.memset(x_scale[:].rearrange("p z c -> p (z c)").bitcast(I32), 0)

        w_passes = w1.rearrange("(z p j) c -> z p j c", z=PASSES, j=PACK)
        nc.sync.dma_start(out=w_raw[0][:], in_=w_passes[0])
        nc.sync.dma_start(
            out=x_scale_table[0:P:4].bitcast(I32),
            in_=x_scales.rearrange("z q c -> q z c").bitcast(I32),
        )
        nc.sync.dma_start(offs_sb[:], offs)
        nc.sync.dma_start(out=w_raw[1][:], in_=w_passes[1])
        load_x(x_first, 0)
        nc.sync.dma_start(ent_sb[:], ent)

        nc.vector.tensor_copy(x_picked_scale[:], x_scale_table[:].indirect(offs_sb[:]))
        first_half, second_half, whole = slice(0, S // 2), slice(S // 2, S), slice(0, S)
        halves = (first_half, second_half)

        for q in range(QUADRANTS):
            nc.sync.dma_start(
                out=x_scale[32 * q : 32 * q + 4].bitcast(I32),
                in_=x_picked_scale[32 * q : 32 * q + 32 : 4].bitcast(I32),
            )
        x_last = loads.tile([P, T], U32, name="x_table1", offset=X_LAST_AT)
        load_x(x_last, 1)
        x_table = [x_first, x_last]

        w_codes, w_scale = [], []
        for z in range(PASSES):
            w_bf = loads.tile(
                [P, PACK, P, PACK], BF16, name=f"w_bf{z}", align_bytes=64, offset=ROUNDED_AT + z * ROW_BYTES
            )
            dealt = w_bf[:].rearrange("p s m j -> p m j s")
            source = w_raw[z][:].rearrange("p j (m s) -> p m j s", s=PACK)
            if z == 1:
                nc.scalar.activation(out=dealt, in_=source, func=ACT.Copy)
            else:
                nc.vector.tensor_copy(dealt, source)
            codes = keep.tile([P, N], U32, name=f"w_codes{z}", align_bytes=64)
            scale = keep.tile([P, N], U8, name=f"w_scale{z}", align_bytes=64)
            nc.vector.quantize_mx(
                out=codes[:].bitcast(FP8X4),
                scales=scale[:],
                in_=w_bf[:].rearrange("p s m j -> p (s m j)"),
            )
            w_codes.append(codes)
            w_scale.append(scale)

        par_rows = par.rearrange("(p s) c -> s p c", s=PACK)
        out_rows = out_0.rearrange("(p s) c -> s p c", s=PACK)
        early = {s: loads.tile([P, U], F32, name=f"early{s}", offset=s * ROW_BYTES) for s in (1, 2)}
        rows_at = (0, ROUNDED_AT, ROUNDED_AT + ROW_BYTES, 3 * ROW_BYTES)
        rows = [loads.tile([P, U], F32, name=f"rows{s}", offset=rows_at[s]) for s in range(PACK)]
        for tile, s in ((rows[0], 0), (early[1], 1), (early[2], 2), (rows[1], 1), (rows[3], 3), (rows[2], 2)):
            nc.sync.dma_start(out=tile[:], in_=par_rows[s])

        x_codes = [keep.tile([P, S], U32, name=f"x_codes{z}", align_bytes=64) for z in range(PASSES)]
        for z in range(PASSES):
            for piece in halves:
                nc.vector.tensor_copy(x_codes[z][:, piece], x_table[z][:].indirect(entries(offs_sb, piece)))

        clipped = [keep.tile([P, 2, S], F32, name=f"clipped{pair}") for pair in range(PACK // 2)]
        for pair in range(PACK // 2):
            for piece in halves:
                y = psum.tile([P, 2, S // 2], F32, name=f"y{pair}_{piece.start}")
                steps = [(z, i) for z in range(PASSES) for i in range(2)]
                for step, (z, i) in enumerate(steps):
                    cols = slice(P * (2 * pair + i), P * (2 * pair + i + 1))
                    nc.tensor.matmul_mx(
                        out=y[:, i, :],
                        lhsT=w_codes[z][:, cols].bitcast(FP8X4),
                        lhsT_scale=w_scale[z][:, cols],
                        rhs=x_codes[z][:, piece].bitcast(FP8X4),
                        rhs_scale=x_scale[:, z, piece],
                        start=(step == 0),
                        stop=(step == len(steps) - 1),
                    )
                nc.vector.tensor_scalar(clipped[pair][:, :, piece], y[:], LIMIT, -LIMIT, ALU.min, ALU.max)

        def window(tile, piece):
            return tile[:].indirect(entries(ent_sb, piece))

        def values(name, piece, at=None):
            shape = [P, piece.stop - piece.start]
            if at is None:
                return keep.tile(shape, F32, name=name)
            return reused.tile(shape, F32, name=name, offset=at)

        def fetch_on_scalar(tile, piece, decayed):
            nc.scalar.activation(out=decayed, in_=window(tile, piece), func=ACT.Copy, scale=DECAY)

        def fetch_on_vector(tile, piece, decayed):
            nc.vector.tensor_scalar(decayed, window(tile, piece), DECAY, 0.0, ALU.mult, ALU.add)

        def subtract(s, piece, new, decayed):
            nc.gpsimd.tensor_tensor(new, decayed, clipped[s // 2][:, s % 2, piece], ALU.subtract)

        def scatter_on_vector(s, piece, new):
            nc.vector.tensor_copy(window(rows[s], piece), new)

        def scatter_on_scalar(s, piece, new):
            nc.scalar.activation(out=window(rows[s], piece), in_=new, func=ACT.Copy)

        def store(s):
            nc.sync.dma_start(out=out_rows[s], in_=rows[s][:])

        decayed_0 = values("decayed_0", whole)
        new_0a = values("new_0a", first_half)
        for piece in halves:
            fetch_on_scalar(rows[0], piece, decayed_0[:, piece])
        subtract(0, first_half, new_0a[:], decayed_0[:, first_half])
        scatter_on_vector(0, first_half, new_0a[:])

        decayed_1 = values("decayed_1", whole)
        new_1 = values("new_1", whole)
        for piece in halves:
            fetch_on_scalar(early[1], piece, decayed_1[:, piece])
            subtract(1, piece, new_1[:, piece], decayed_1[:, piece])
        decayed_2 = values("decayed_2", whole)
        new_2 = values("new_2", whole)
        fetch_on_scalar(early[2], whole, decayed_2[:])
        subtract(2, whole, new_2[:], decayed_2[:])
        scatter_on_scalar(1, whole, new_1[:])
        store(1)

        decayed_3 = values("decayed_3", whole, 0)
        new_3 = values("new_3", whole)
        for piece in halves:
            fetch_on_vector(rows[3], piece, decayed_3[:, piece])
            subtract(3, piece, new_3[:, piece], decayed_3[:, piece])
        scatter_on_vector(2, whole, new_2[:])
        store(2)
        scatter_on_scalar(3, whole, new_3[:])

        new_0b = values("new_0b", second_half, 0)
        subtract(0, second_half, new_0b[:], decayed_0[:, second_half])
        scatter_on_vector(0, second_half, new_0b[:])
        planes = reused.tile([P, 2, PACK, U // 2], BF16, name="planes", offset=HALF_BYTES)
        for s in (1, 2):
            halved = rows[s][:].rearrange("p (h c) -> p h c", h=2)
            nc.gpsimd.tensor_scalar(planes[:, :, s, :], halved, 1.0, 1.0, ALU.mult, ALU.mult)
        store(3)
        store(0)
        nc.vector.tensor_copy(planes[:, 0, 3, :], rows[3][:, : U // 2])
        for first in (0, CHUNK):
            nc.vector.tensor_copy(planes[:, 0, 0, first : first + CHUNK], rows[0][:, first : first + CHUNK])
        for s in (3, 0):
            nc.scalar.copy(planes[:, 1, s, :], rows[s][:, U // 2 :])

        grouped = keep.tile([P, U, PACK], BF16, name="grouped", align_bytes=64)

        def weave(copy, first, stop):
            h, origin = first // (U // 2), first // (U // 2) * (U // 2)
            copy(
                out=grouped[:, first:stop, :].rearrange("p (c i) s -> p c s i", i=NEAR),
                in_=planes[:, h, :, first - origin : stop - origin].rearrange("p s (c i) -> p c s i", i=NEAR),
            )

        out_codes = keep.tile([P, U], U32, name="out_codes", align_bytes=64)
        out_scale = keep.tile([P, U], U8, name="out_scale", align_bytes=64)
        out_words = out_1[0].rearrange("p c r -> p (c r)").bitcast(I32)

        def quantise(first, stop):
            nc.vector.quantize_mx(
                out=out_codes[:, first:stop].bitcast(FP8X4),
                scales=out_scale[:, first:stop],
                in_=grouped[:, first:stop, :].rearrange("p c s -> p (c s)"),
            )

        def store_codes(first, stop):
            nc.sync.dma_start(out=out_words[:, first:stop], in_=out_codes[:, first:stop].bitcast(I32))

        for first in (0, CHUNK):
            weave(nc.vector.tensor_copy, first, first + CHUNK)
        for first in (0, CHUNK):
            quantise(first, first + CHUNK)
        store_codes(0, 2 * CHUNK)
        weave(nc.scalar.copy, 2 * CHUNK, 3 * CHUNK)
        weave(nc.vector.tensor_copy, 3 * CHUNK, SCALAR_LAST)
        weave(nc.scalar.copy, SCALAR_LAST, U)
        for first in (2 * CHUNK, 3 * CHUNK):
            quantise(first, first + CHUNK)
            store_codes(first, first + CHUNK)
        for q in range(QUADRANTS):
            queue = nc.scalar if q % 2 else nc.sync
            queue.dma_start(
                out=out_2[0, 4 * q : 4 * q + 4, :].bitcast(I32),
                in_=out_scale[32 * q : 32 * q + 4, :].bitcast(I32),
            )
